import numpy as np
import ml_dtypes


def mxq(x, axis, fmt="e4m3"):
    dtype, down = {"e4m3": (ml_dtypes.float8_e4m3fn, 7), "e5m2": (ml_dtypes.float8_e5m2, 14)}[fmt]
    v = np.moveaxis(np.asarray(x, np.float32).astype(ml_dtypes.bfloat16).astype(np.float64), axis, -1)
    blocks = v.reshape(v.shape[:-1] + (-1, 32))
    amax = np.abs(blocks).max(-1, keepdims=True)
    byte = np.maximum(np.where(amax > 0, np.frexp(amax)[1] - 1 + 127, 0) - down, 1)
    scale = np.exp2(byte - 127.0)
    codes = (blocks / scale).astype(np.float32).astype(dtype).astype(np.float64)
    return np.moveaxis((codes * scale).reshape(v.shape), -1, axis)


WIDE = False


def mx_kscale(k):
    if not WIDE:
        return np.ones(k)
    levels = np.array([10, -10, 5, -5, 0])
    if k % 512:
        return np.exp2(np.random.permutation(np.resize(levels, k // 32))).repeat(32)
    a = np.empty((k // 512, 16))
    for p in range(k // 512):
        a[p, :8] = np.random.permutation(np.resize(levels, 8))
        for g in range(8):
            far = levels[np.abs(levels - a[p, g]) >= 10]
            a[p, g + 8] = far[np.random.randint(len(far))]
    return np.exp2(a.ravel()).repeat(32)


def f64(x):
    return np.asarray(x).astype(np.float64)


def striped(idx):
    return np.tile(idx.reshape(-1, 16).T, (8, 1)).astype(np.uint16)


def unstriped(offs):
    return offs[:16].T.reshape(-1).astype(np.int64)


E2M1 = np.array([0.0, 0.5, 1.0, 1.5, 2.0, 3.0, 4.0, 6.0, -0.0, -0.5, -1.0, -1.5, -2.0, -3.0, -4.0, -6.0])


def pack_fp4(w):
    k, n = w.shape
    w = f64(np.asarray(w, np.float32).astype(ml_dtypes.bfloat16)).reshape(k // 32, 32, n)
    amax = np.abs(w).max(1)
    mant, ex = np.frexp(amax / 6.0)
    byte = np.clip(np.where(amax > 0, np.where(mant > 0.5, ex, ex - 1) + 127, 1), 1, 254)
    scaled = (w * np.exp2(127.0 - byte)[:, None, :]).reshape(k, n).astype(np.float32)
    c = np.ascontiguousarray(scaled.reshape(k // 512, 128, 4, n).transpose(0, 1, 3, 2)).astype(ml_dtypes.float4_e2m1fn).view(np.uint8) & 0xF
    words = (c[..., 0::2] | (c[..., 1::2] << 4)).reshape(k // 512, 128, 2 * n)
    return np.ascontiguousarray(words), np.ascontiguousarray(byte.astype(np.uint8).reshape(k // 512, 16, n))


def unpack_fp4(words, scales):
    g, _, n = scales.shape
    words = np.ascontiguousarray(words).reshape(g, 128, n, 2)
    nib = np.empty((g, 128, n, 4), np.uint8)
    nib[..., 0::2] = words & 0xF
    nib[..., 1::2] = words >> 4
    vals = E2M1[nib] * np.repeat(np.exp2(scales.astype(np.float64) - 127.0), 8, axis=1)[..., None]
    return vals.transpose(0, 1, 3, 2).reshape(g * 512, n)


def silu(v):
    return v / (1.0 + np.exp(-np.maximum(v, -700.0)))


K, T, S, N, U = 512, 2048, 1024, 128, 1024


def setup_inputs():
    n = np.random.standard_normal
    s = mx_kscale(K)[:, None]
    packed_w1 = pack_fp4(n((K, N)) / np.sqrt(K) / s)
    return {
        "xT": (n((K, T)) * s).astype(np.float32),
        "w1_words": packed_w1[0],
        "w1_scales": packed_w1[1],
        "gamma": np.random.uniform(0.5, 1.5, (N, U)).astype(np.float32),
        "beta": (0.5 * n((N, U))).astype(np.float32),
        "offs": striped(np.random.permutation(T)[:S]),
        "cls": striped(np.random.randint(0, U, S)),
    }


def reference(xT, w1_words, w1_scales, gamma, beta, offs, cls):
    xq = mxq(f64(xT)[:, unstriped(offs)], 0, "e4m3")
    y = unpack_fp4(w1_words, w1_scales).T @ xq
    g = f64(gamma)[:, unstriped(cls)]
    s = f64(beta)[:, unstriped(cls)]
    return silu(y * g + s)

@@ -1,0 +1,152 @@
+from contextlib import ExitStack
+
+import concourse.mybir as mybir
+
+K, T, S, N, U = 512, 2048, 1024, 128, 1024
+FLOPS = 2 * K * N * S
+
+F32 = mybir.dt.float32
+BF16 = mybir.dt.bfloat16
+I32 = mybir.dt.int32
+U32 = mybir.dt.uint32
+U16 = mybir.dt.uint16
+U8 = mybir.dt.uint8
+FP8X4 = mybir.dt.float8_e4m3fn_x4
+FP4X4 = mybir.dt.float4_e2m1fn_x4
+ACT = mybir.ActivationFunctionType
+ALU = mybir.AluOpType
+
+P = 128
+PIECE = 256
+CLASS_PIECE = 512
+PAIR_CHUNKS = (1024, 512, 512)
+ROW2_CHUNKS = (1024, 1024)
+ROW3_CHUNKS = (1024, 768, 256)
+
+
+def spans(widths):
+    result, start = [], 0
+    for width in widths:
+        result.append((start, start + width))
+        start = start + width
+    return result
+
+
+def tile_picked_cbn_silu_e_kernel(tc, xT, w1_words, w1_scales, gamma, beta, offs, cls, out):
+    nc = tc.nc
+    pieces = S // PIECE
+    x_rows = xT.rearrange("(p j) t -> p j t", j=4)
+
+    with ExitStack() as ctx:
+        keep = ctx.enter_context(tc.tile_pool(name="keep", bufs=1))
+        psum = ctx.enter_context(tc.psum_pool(name="psum", bufs=1))
+
+        cls_sb = keep.tile([P, S // 16], U16, name="cls_sb")
+        offs_sb = keep.tile([P, S // 16], U16, name="offs_sb")
+        gamma_sb = keep.tile([P, U], F32, name="gamma_sb")
+        beta_sb = keep.tile([P, U], F32, name="beta_sb")
+
+        nc.sync.dma_start(cls_sb[:], cls)
+        nc.sync.dma_start(gamma_sb[:], gamma)
+        nc.sync.dma_start(beta_sb[:], beta)
+        nc.sync.dma_start(offs_sb[:], offs)
+
+        row2_raw, pair_raw, row3_raw = [], [], []
+        for c, (a, b) in enumerate(spans(ROW2_CHUNKS)):
+            raw = keep.tile([P, b - a], F32, name="row2_raw%d" % c)
+            nc.sync.dma_start(raw[:], x_rows[:, 2, a:b])
+            row2_raw.append(raw)
+        w_codes = keep.tile([P, 2 * N], U8, name="w_codes", align_bytes=64)
+        w_scale = keep.tile([P, N], U8, name="w_scale", align_bytes=64)
+        nc.gpsimd.memset(w_scale[:], 0)
+        nc.sync.dma_start(w_codes[:].bitcast(I32), w1_words[0].bitcast(I32))
+        for q in range(4):
+            nc.sync.dma_start(w_scale[32 * q : 32 * q + 4, :].bitcast(I32), w1_scales[0, 4 * q : 4 * q + 4, :].bitcast(I32))
+
+        for c, (a, b) in enumerate(spans(PAIR_CHUNKS)):
+            raw = keep.tile([P, 2, b - a], F32, name="pair_raw%d" % c)
+            nc.sync.dma_start(raw[:], x_rows[:, 0:2, a:b])
+            pair_raw.append(raw)
+        for c, (a, b) in enumerate(spans(ROW3_CHUNKS)):
+            raw = keep.tile([P, b - a], F32, name="row3_raw%d" % c)
+            nc.sync.dma_start(raw[:], x_rows[:, 3, a:b])
+            row3_raw.append(raw)
+
+        zero_in = keep.tile([P, 1], F32, name="zero_in")
+        zero_bias = keep.tile([P, 1], F32, name="zero_bias")
+        nc.gpsimd.memset(zero_in[:], 0.0)
+        nc.scalar.activation(zero_bias[:], zero_in[:], ACT.Silu)
+
+        gamma_pick = keep.tile([P, S], F32, name="gamma_pick")
+        beta_pick = keep.tile([P, S], F32, name="beta_pick")
+        for table, pick in ((gamma_sb, gamma_pick), (beta_sb, beta_pick)):
+            for a in range(0, S, CLASS_PIECE):
+                entries = cls_sb[:, a // 16 : (a + CLASS_PIECE) // 16]
+                nc.vector.tensor_copy(pick[:, a : a + CLASS_PIECE], table[:].indirect(entries))
+
+        woven = [keep.tile([P, PIECE, 4], BF16, name="woven%d" % i, align_bytes=64) for i in range(pieces)]
+
+        def entries_of(i):
+            return offs_sb[:, i * PIECE // 16 : (i + 1) * PIECE // 16]
+
+        row2 = keep.tile([P, T], BF16, name="row2")
+        for raw, (a, b) in zip(row2_raw, spans(ROW2_CHUNKS)):
+            nc.scalar.copy(row2[:, a:b], raw[:])
+        for i in range(pieces):
+            nc.scalar.activation(woven[i][:, :, 2], row2[:].indirect(entries_of(i)), ACT.Copy)
+
+        pair = keep.tile([P, T, 2], BF16, name="pair")
+        for raw, (a, b) in zip(pair_raw, spans(PAIR_CHUNKS)):
+            nc.vector.tensor_copy(pair[:, a:b, :], raw[:].rearrange("p j t -> p t j"))
+        pair_words = pair[:].rearrange("p t j -> p (t j)").bitcast(U32)
+        for i in range(pieces):
+            words = woven[i][:].rearrange("p n j -> p (n j)").bitcast(U32).rearrange("p (n u) -> p n u", u=2)
+            nc.vector.tensor_copy(words[:, :, 0], pair_words.indirect(entries_of(i)))
+
+        row3 = keep.tile([P, T], BF16, name="row3")
+        for raw, (a, b) in zip(row3_raw, spans(ROW3_CHUNKS)):
+            nc.scalar.copy(row3[:, a:b], raw[:])
+        for i in range(pieces):
+            nc.scalar.activation(woven[i][:, :, 3], row3[:].indirect(entries_of(i)), ACT.Copy)
+
+        steps = [(0, 0, 256), (1, 0, 256), (2, 0, 256), (3, 0, 128), (3, 128, 256)]
+        banks = [psum.tile([P, b - a], F32, name="bank%d" % s) for s, (i, a, b) in enumerate(steps)]
+        scaled = [keep.tile([P, b - a], F32, name="scaled%d" % s) for s, (i, a, b) in enumerate(steps)]
+
+        def columns(s):
+            i, a, b = steps[s]
+            return slice(i * PIECE + a, i * PIECE + b)
+
+        def product(s):
+            i, a, b = steps[s]
+            codes = keep.tile([P, b - a], U32, name="codes%d" % s, align_bytes=64)
+            scales = keep.tile([P, b - a], U8, name="scales%d" % s, align_bytes=64)
+            nc.vector.quantize_mx(out=codes[:].bitcast(FP8X4), scales=scales[:], in_=woven[i][:, a:b, :].rearrange("p n j -> p (n j)"))
+            nc.tensor.matmul_mx(
+                out=banks[s][:],
+                lhsT=w_codes[:].bitcast(FP4X4),
+                lhsT_scale=w_scale[:],
+                rhs=codes[:].bitcast(FP8X4),
+                rhs_scale=scales[:],
+                start=True,
+                stop=True,
+            )
+
+        def scale(s):
+            nc.vector.tensor_tensor(scaled[s][:], banks[s][:], gamma_pick[:, columns(s)], ALU.mult)
+
+        def finish(s):
+            i, a, b = steps[s]
+            shifted = keep.tile([P, b - a], F32, name="shifted%d" % s)
+            result = keep.tile([P, b - a], F32, name="result%d" % s)
+            nc.vector.tensor_tensor(shifted[:], scaled[s][:], beta_pick[:, columns(s)], ALU.add)
+            nc.scalar.activation(result[:], shifted[:], ACT.Silu, bias=zero_bias[:])
+            nc.sync.dma_start(out[:, columns(s)], result[:])
+
+        for s in range(len(steps) + 2):
+            if s < len(steps):
+                product(s)
+            if 0 <= s - 1 < len(steps):
+                scale(s - 1)
+            if 0 <= s - 2 < len(steps):
+                finish(s - 2)

@@ -1,6 +1,7 @@
 from contextlib import ExitStack
 
 import concourse.mybir as mybir
+from concourse.masks import make_identity
 
 K, T, S, N, U = 512, 2048, 1024, 128, 1024
 FLOPS = 2 * K * N * S
@@ -17,11 +18,11 @@ ACT = mybir.ActivationFunctionType
 ALU = mybir.AluOpType
 
 P = 128
-PIECE = 256
 CLASS_PIECE = 512
-PAIR_CHUNKS = (1024, 512, 512)
-ROW2_CHUNKS = (1024, 1024)
-ROW3_CHUNKS = (1024, 768, 256)
+PIECES = (256, 256, 256, 256)
+PARTS = (256, 256, 256, 128, 128)
+LOW_CHUNKS = ((1024, 512), (1024, 640))
+HIGH_CHUNKS = ((1024, 0), (512, 512), (512, 320))
 
 
 def spans(widths):
@@ -34,8 +35,9 @@ def spans(widths):
 
 def tile_picked_cbn_silu_e_kernel(tc, xT, w1_words, w1_scales, gamma, beta, offs, cls, out):
     nc = tc.nc
-    pieces = S // PIECE
     x_rows = xT.rearrange("(p j) t -> p j t", j=4)
+    pieces = spans(PIECES)
+    parts = spans(PARTS)
 
     with ExitStack() as ctx:
         keep = ctx.enter_context(tc.tile_pool(name="keep", bufs=1))
@@ -48,14 +50,21 @@ def tile_picked_cbn_silu_e_kernel(tc, xT, w1_words, w1_scales, gamma, beta, offs
 
         nc.sync.dma_start(cls_sb[:], cls)
         nc.sync.dma_start(gamma_sb[:], gamma)
-        nc.sync.dma_start(beta_sb[:], beta)
-        nc.sync.dma_start(offs_sb[:], offs)
 
-        row2_raw, pair_raw, row3_raw = [], [], []
-        for c, (a, b) in enumerate(spans(ROW2_CHUNKS)):
-            raw = keep.tile([P, b - a], F32, name="row2_raw%d" % c)
-            nc.sync.dma_start(raw[:], x_rows[:, 2, a:b])
-            row2_raw.append(raw)
+        def load_pair(u, chunks):
+            tiles = []
+            for c, (a, b) in enumerate(spans([width for width, share in chunks])):
+                raw = keep.tile([P, 2, b - a], F32, name="raw%d_%d" % (u, c))
+                nc.sync.dma_start(raw[:], x_rows[:, 2 * u : 2 * u + 2, a:b])
+                tiles.append(raw)
+                if u == 0 and c == 0:
+                    nc.sync.dma_start(beta_sb[:], beta)
+                    nc.sync.dma_start(offs_sb[:], offs)
+            return tiles
+
+        low_raw = load_pair(0, LOW_CHUNKS)
+        high_raw = load_pair(1, HIGH_CHUNKS)
+
         w_codes = keep.tile([P, 2 * N], U8, name="w_codes", align_bytes=64)
         w_scale = keep.tile([P, N], U8, name="w_scale", align_bytes=64)
         nc.gpsimd.memset(w_scale[:], 0)
@@ -63,90 +72,86 @@ def tile_picked_cbn_silu_e_kernel(tc, xT, w1_words, w1_scales, gamma, beta, offs
         for q in range(4):
             nc.sync.dma_start(w_scale[32 * q : 32 * q + 4, :].bitcast(I32), w1_scales[0, 4 * q : 4 * q + 4, :].bitcast(I32))
 
-        for c, (a, b) in enumerate(spans(PAIR_CHUNKS)):
-            raw = keep.tile([P, 2, b - a], F32, name="pair_raw%d" % c)
-            nc.sync.dma_start(raw[:], x_rows[:, 0:2, a:b])
-            pair_raw.append(raw)
-        for c, (a, b) in enumerate(spans(ROW3_CHUNKS)):
-            raw = keep.tile([P, b - a], F32, name="row3_raw%d" % c)
-            nc.sync.dma_start(raw[:], x_rows[:, 3, a:b])
-            row3_raw.append(raw)
-
         zero_in = keep.tile([P, 1], F32, name="zero_in")
         zero_bias = keep.tile([P, 1], F32, name="zero_bias")
         nc.gpsimd.memset(zero_in[:], 0.0)
         nc.scalar.activation(zero_bias[:], zero_in[:], ACT.Silu)
+        ident = keep.tile([P, P], F32, name="ident")
+        make_identity(nc, ident[:])
 
         gamma_pick = keep.tile([P, S], F32, name="gamma_pick")
         beta_pick = keep.tile([P, S], F32, name="beta_pick")
         for table, pick in ((gamma_sb, gamma_pick), (beta_sb, beta_pick)):
             for a in range(0, S, CLASS_PIECE):
-                entries = cls_sb[:, a // 16 : (a + CLASS_PIECE) // 16]
-                nc.vector.tensor_copy(pick[:, a : a + CLASS_PIECE], table[:].indirect(entries))
+                nc.vector.tensor_copy(pick[:, a : a + CLASS_PIECE], table[:].indirect(cls_sb[:, a // 16 : (a + CLASS_PIECE) // 16]))
 
-        woven = [keep.tile([P, PIECE, 4], BF16, name="woven%d" % i, align_bytes=64) for i in range(pieces)]
+        picked = [keep.tile([P, 2, b - a], U32, name="picked%d" % i) for i, (a, b) in enumerate(pieces)]
+        woven = [keep.tile([P, b - a, 4], BF16, name="woven%d" % i, align_bytes=64) for i, (a, b) in enumerate(pieces)]
 
-        def entries_of(i):
-            return offs_sb[:, i * PIECE // 16 : (i + 1) * PIECE // 16]
+        def round_pair(u, chunks, tiles):
+            pair = keep.tile([P, T, 2], BF16, name="pair%d" % u)
+            for raw, (width, share), (a, b) in zip(tiles, chunks, spans([width for width, share in chunks])):
+                if share < width:
+                    nc.scalar.copy(pair[:, a + share : b, :], raw[:, :, share:].rearrange("p j t -> p t j"))
+                if share > 0:
+                    nc.vector.tensor_copy(pair[:, a : a + share, :], raw[:, :, :share].rearrange("p j t -> p t j"))
+            return pair
 
-        row2 = keep.tile([P, T], BF16, name="row2")
-        for raw, (a, b) in zip(row2_raw, spans(ROW2_CHUNKS)):
-            nc.scalar.copy(row2[:, a:b], raw[:])
-        for i in range(pieces):
-            nc.scalar.activation(woven[i][:, :, 2], row2[:].indirect(entries_of(i)), ACT.Copy)
+        def gather_pair(u, pair, i):
+            a, b = pieces[i]
+            window = pair[:].rearrange("p t j -> p (t j)").bitcast(U32)
+            nc.vector.tensor_copy(picked[i][:, u, :], window.indirect(offs_sb[:, a // 16 : b // 16]))
 
-        pair = keep.tile([P, T, 2], BF16, name="pair")
-        for raw, (a, b) in zip(pair_raw, spans(PAIR_CHUNKS)):
-            nc.vector.tensor_copy(pair[:, a:b, :], raw[:].rearrange("p j t -> p t j"))
-        pair_words = pair[:].rearrange("p t j -> p (t j)").bitcast(U32)
-        for i in range(pieces):
+        def turn(pick, name):
+            turned = keep.tile([P, S], F32, name=name)
+            for a in range(0, S, CLASS_PIECE):
+                bank = psum.tile([P, CLASS_PIECE], F32, name="turn_bank", tag="work", bufs=3)
+                for c in range(0, CLASS_PIECE, P):
+                    nc.tensor.transpose(bank[:, c : c + P], pick[:, a + c : a + c + P], ident[:])
+                nc.scalar.copy(turned[:, a : a + CLASS_PIECE], bank[:])
+            return turned
+
+        gamma_turned = turn(gamma_pick, "gamma_turned")
+
+        low = round_pair(0, LOW_CHUNKS, low_raw)
+        beta_turned = turn(beta_pick, "beta_turned")
+        sums = [psum.tile([P, b - a], F32, name="sum%d" % s) for s, (a, b) in enumerate(parts)]
+        for s, (a, b) in enumerate(parts):
+            for c in range(a, b, P):
+                nc.tensor.matmul(sums[s][:, c - a : c - a + P], lhsT=beta_turned[:, c : c + P], rhs=ident[:], is_transpose=True, start=(c == a), stop=False)
+        for i in range(len(pieces)):
+            gather_pair(0, low, i)
+        high = round_pair(1, HIGH_CHUNKS, high_raw)
+        for i in range(len(pieces)):
+            gather_pair(1, high, i)
             words = woven[i][:].rearrange("p n j -> p (n j)").bitcast(U32).rearrange("p (n u) -> p n u", u=2)
-            nc.vector.tensor_copy(words[:, :, 0], pair_words.indirect(entries_of(i)))
+            nc.scalar.copy(words, picked[i][:].rearrange("p u n -> p n u"))
 
-        row3 = keep.tile([P, T], BF16, name="row3")
-        for raw, (a, b) in zip(row3_raw, spans(ROW3_CHUNKS)):
-            nc.scalar.copy(row3[:, a:b], raw[:])
-        for i in range(pieces):
-            nc.scalar.activation(woven[i][:, :, 3], row3[:].indirect(entries_of(i)), ACT.Copy)
+        banks = []
+        for i, (first, last) in enumerate(pieces):
+            codes = keep.tile([P, last - first], U32, name="codes%d" % i, align_bytes=64)
+            scales = keep.tile([P, last - first], U8, name="scales%d" % i, align_bytes=64)
+            nc.vector.quantize_mx(out=codes[:].bitcast(FP8X4), scales=scales[:], in_=woven[i][:].rearrange("p n j -> p (n j)"))
+            for a, b in parts:
+                if first <= a < last:
+                    bank = psum.tile([P, b - a], F32, name="mx_bank", tag="work", bufs=3)
+                    banks.append(bank)
+                    for c in range(a, b, P):
+                        nc.tensor.matmul_mx(
+                            out=bank[:, c - a : c - a + P],
+                            lhsT=codes[:, c - first : c - first + P].bitcast(FP8X4),
+                            lhsT_scale=scales[:, c - first : c - first + P],
+                            rhs=w_codes[:].bitcast(FP4X4),
+                            rhs_scale=w_scale[:],
+                            start=True,
+                            stop=True,
+                        )
 
-        steps = [(0, 0, 256), (1, 0, 256), (2, 0, 256), (3, 0, 128), (3, 128, 256)]
-        banks = [psum.tile([P, b - a], F32, name="bank%d" % s) for s, (i, a, b) in enumerate(steps)]
-        scaled = [keep.tile([P, b - a], F32, name="scaled%d" % s) for s, (i, a, b) in enumerate(steps)]
-
-        def columns(s):
-            i, a, b = steps[s]
-            return slice(i * PIECE + a, i * PIECE + b)
-
-        def product(s):
-            i, a, b = steps[s]
-            codes = keep.tile([P, b - a], U32, name="codes%d" % s, align_bytes=64)
-            scales = keep.tile([P, b - a], U8, name="scales%d" % s, align_bytes=64)
-            nc.vector.quantize_mx(out=codes[:].bitcast(FP8X4), scales=scales[:], in_=woven[i][:, a:b, :].rearrange("p n j -> p (n j)"))
-            nc.tensor.matmul_mx(
-                out=banks[s][:],
-                lhsT=w_codes[:].bitcast(FP4X4),
-                lhsT_scale=w_scale[:],
-                rhs=codes[:].bitcast(FP8X4),
-                rhs_scale=scales[:],
-                start=True,
-                stop=True,
-            )
-
-        def scale(s):
-            nc.vector.tensor_tensor(scaled[s][:], banks[s][:], gamma_pick[:, columns(s)], ALU.mult)
-
-        def finish(s):
-            i, a, b = steps[s]
-            shifted = keep.tile([P, b - a], F32, name="shifted%d" % s)
+        for s, (a, b) in enumerate(parts):
+            scaled = keep.tile([P, b - a], F32, name="scaled%d" % s)
             result = keep.tile([P, b - a], F32, name="result%d" % s)
-            nc.vector.tensor_tensor(shifted[:], scaled[s][:], beta_pick[:, columns(s)], ALU.add)
-            nc.scalar.activation(result[:], shifted[:], ACT.Silu, bias=zero_bias[:])
-            nc.sync.dma_start(out[:, columns(s)], result[:])
-
-        for s in range(len(steps) + 2):
-            if s < len(steps):
-                product(s)
-            if 0 <= s - 1 < len(steps):
-                scale(s - 1)
-            if 0 <= s - 2 < len(steps):
-                finish(s - 2)
+            nc.vector.tensor_tensor(scaled[:], banks[s][:], gamma_turned[:, a:b], ALU.mult)
+            for c in range(a, b, P):
+                nc.tensor.matmul(sums[s][:, c - a : c - a + P], lhsT=scaled[:, c - a : c - a + P], rhs=ident[:], is_transpose=True, start=False, stop=(c + P == b))
+            nc.scalar.activation(result[:], sums[s][:], ACT.Silu, bias=zero_bias[:])
+            nc.sync.dma_start(out[:, a:b], result[:])

@@ -20,9 +20,11 @@ ALU = mybir.AluOpType
 P = 128
 CLASS_PIECE = 512
 PIECES = (256, 256, 256, 256)
-PARTS = (256, 256, 256, 128, 128)
-LOW_CHUNKS = ((1024, 512), (1024, 640))
-HIGH_CHUNKS = ((1024, 0), (512, 512), (512, 320))
+SHEETS = (256, 256, 256, 128, 128)
+BANKS = (384, 512, 128)
+PARTS = (128, 256, 256, 256, 128)
+LOW_CHUNKS = ((1024, 0), (1024, 608))
+HIGH_CHUNKS = ((512, 0), (768, 0), (512, 512), (256, 96))
 
 
 def spans(widths):
@@ -37,6 +39,7 @@ def tile_picked_cbn_silu_e_kernel(tc, xT, w1_words, w1_scales, gamma, beta, offs
     nc = tc.nc
     x_rows = xT.rearrange("(p j) t -> p j t", j=4)
     pieces = spans(PIECES)
+    sheets = spans(SHEETS)
     parts = spans(PARTS)
 
     with ExitStack() as ctx:
@@ -50,6 +53,8 @@ def tile_picked_cbn_silu_e_kernel(tc, xT, w1_words, w1_scales, gamma, beta, offs
 
         nc.sync.dma_start(cls_sb[:], cls)
         nc.sync.dma_start(gamma_sb[:], gamma)
+        nc.sync.dma_start(beta_sb[:], beta)
+        nc.sync.dma_start(offs_sb[:], offs)
 
         def load_pair(u, chunks):
             tiles = []
@@ -57,9 +62,6 @@ def tile_picked_cbn_silu_e_kernel(tc, xT, w1_words, w1_scales, gamma, beta, offs
                 raw = keep.tile([P, 2, b - a], F32, name="raw%d_%d" % (u, c))
                 nc.sync.dma_start(raw[:], x_rows[:, 2 * u : 2 * u + 2, a:b])
                 tiles.append(raw)
-                if u == 0 and c == 0:
-                    nc.sync.dma_start(beta_sb[:], beta)
-                    nc.sync.dma_start(offs_sb[:], offs)
             return tiles
 
         low_raw = load_pair(0, LOW_CHUNKS)
@@ -79,17 +81,22 @@ def tile_picked_cbn_silu_e_kernel(tc, xT, w1_words, w1_scales, gamma, beta, offs
         ident = keep.tile([P, P], F32, name="ident")
         make_identity(nc, ident[:])
 
-        gamma_pick = keep.tile([P, S], F32, name="gamma_pick")
-        beta_pick = keep.tile([P, S], F32, name="beta_pick")
-        for table, pick in ((gamma_sb, gamma_pick), (beta_sb, beta_pick)):
+        def look_up(table, name):
+            halves = []
             for a in range(0, S, CLASS_PIECE):
-                nc.vector.tensor_copy(pick[:, a : a + CLASS_PIECE], table[:].indirect(cls_sb[:, a // 16 : (a + CLASS_PIECE) // 16]))
+                pick = keep.tile([P, CLASS_PIECE], F32, name="%s%d" % (name, a // CLASS_PIECE))
+                nc.vector.tensor_copy(pick[:], table[:].indirect(cls_sb[:, a // 16 : (a + CLASS_PIECE) // 16]))
+                halves.append(pick)
+            return halves
+
+        gamma_pick = look_up(gamma_sb, "gamma_pick")
+        beta_pick = look_up(beta_sb, "beta_pick")
 
         picked = [keep.tile([P, 2, b - a], U32, name="picked%d" % i) for i, (a, b) in enumerate(pieces)]
-        woven = [keep.tile([P, b - a, 4], BF16, name="woven%d" % i, align_bytes=64) for i, (a, b) in enumerate(pieces)]
+        woven = [keep.tile([P, b - a, 4], BF16, name="woven%d" % i, align_bytes=64) for i, (a, b) in enumerate(sheets)]
 
-        def round_pair(u, chunks, tiles):
-            pair = keep.tile([P, T, 2], BF16, name="pair%d" % u)
+        def round_pair(name, chunks, tiles):
+            pair = keep.tile([P, T, 2], BF16, name=name)
             for raw, (width, share), (a, b) in zip(tiles, chunks, spans([width for width, share in chunks])):
                 if share < width:
                     nc.scalar.copy(pair[:, a + share : b, :], raw[:, :, share:].rearrange("p j t -> p t j"))
@@ -102,41 +109,46 @@ def tile_picked_cbn_silu_e_kernel(tc, xT, w1_words, w1_scales, gamma, beta, offs
             window = pair[:].rearrange("p t j -> p (t j)").bitcast(U32)
             nc.vector.tensor_copy(picked[i][:, u, :], window.indirect(offs_sb[:, a // 16 : b // 16]))
 
-        def turn(pick, name):
-            turned = keep.tile([P, S], F32, name=name)
-            for a in range(0, S, CLASS_PIECE):
-                bank = psum.tile([P, CLASS_PIECE], F32, name="turn_bank", tag="work", bufs=3)
-                for c in range(0, CLASS_PIECE, P):
-                    nc.tensor.transpose(bank[:, c : c + P], pick[:, a + c : a + c + P], ident[:])
-                nc.scalar.copy(turned[:, a : a + CLASS_PIECE], bank[:])
-            return turned
+        def turn(pick, turned, copy):
+            bank = psum.tile([P, CLASS_PIECE], F32, name="turn_bank", tag="work", bufs=3)
+            for c in range(0, CLASS_PIECE, P):
+                nc.tensor.transpose(bank[:, c : c + P], pick[:, c : c + P], ident[:])
+            copy(turned, bank[:])
 
-        gamma_turned = turn(gamma_pick, "gamma_turned")
+        gamma_turned = keep.tile([P, S], F32, name="gamma_turned")
+        turn(gamma_pick[0], gamma_turned[:, :CLASS_PIECE], nc.scalar.copy)
+        turn(gamma_pick[1], gamma_turned[:, CLASS_PIECE:], nc.vector.tensor_copy)
 
-        low = round_pair(0, LOW_CHUNKS, low_raw)
-        beta_turned = turn(beta_pick, "beta_turned")
+        low = round_pair("gamma_pick0", LOW_CHUNKS, low_raw)
+        for i in range(len(pieces)):
+            gather_pair(0, low, i)
+        beta_turned = [keep.tile([P, CLASS_PIECE], F32, name="raw0_1")]
+        turn(beta_pick[0], beta_turned[0][:], nc.scalar.copy)
+        high = round_pair("high", HIGH_CHUNKS, high_raw)
+        beta_turned.append(keep.tile([P, CLASS_PIECE], F32, name="raw1_%d" % (len(HIGH_CHUNKS) - 1)))
+        turn(beta_pick[1], beta_turned[1][:], nc.scalar.copy)
         sums = [psum.tile([P, b - a], F32, name="sum%d" % s) for s, (a, b) in enumerate(parts)]
         for s, (a, b) in enumerate(parts):
             for c in range(a, b, P):
-                nc.tensor.matmul(sums[s][:, c - a : c - a + P], lhsT=beta_turned[:, c : c + P], rhs=ident[:], is_transpose=True, start=(c == a), stop=False)
-        for i in range(len(pieces)):
-            gather_pair(0, low, i)
-        high = round_pair(1, HIGH_CHUNKS, high_raw)
+                half, at = divmod(c, CLASS_PIECE)
+                nc.tensor.matmul(sums[s][:, c - a : c - a + P], lhsT=beta_turned[half][:, at : at + P], rhs=ident[:], is_transpose=True, start=(c == a), stop=False)
         for i in range(len(pieces)):
             gather_pair(1, high, i)
-            words = woven[i][:].rearrange("p n j -> p (n j)").bitcast(U32).rearrange("p (n u) -> p n u", u=2)
-            nc.scalar.copy(words, picked[i][:].rearrange("p u n -> p n u"))
-
-        banks = []
-        for i, (first, last) in enumerate(pieces):
-            codes = keep.tile([P, last - first], U32, name="codes%d" % i, align_bytes=64)
-            scales = keep.tile([P, last - first], U8, name="scales%d" % i, align_bytes=64)
-            nc.vector.quantize_mx(out=codes[:].bitcast(FP8X4), scales=scales[:], in_=woven[i][:].rearrange("p n j -> p (n j)"))
-            for a, b in parts:
+            first, last = pieces[i]
+            for w, (a, b) in enumerate(sheets):
                 if first <= a < last:
-                    bank = psum.tile([P, b - a], F32, name="mx_bank", tag="work", bufs=3)
-                    banks.append(bank)
-                    for c in range(a, b, P):
+                    words = woven[w][:].rearrange("p n j -> p (n j)").bitcast(U32).rearrange("p (n u) -> p n u", u=2)
+                    nc.scalar.copy(words, picked[i][:, :, a - first : b - first].rearrange("p u n -> p n u"))
+
+        banks = [psum.tile([P, b - a], F32, name="mx_bank", tag="work", bufs=3) for a, b in spans(BANKS)]
+        def quantise(w):
+            first, last = sheets[w]
+            codes = keep.tile([P, last - first], U32, name="codes%d" % w, align_bytes=64)
+            scales = keep.tile([P, last - first], U8, name="scales%d" % w, align_bytes=64)
+            nc.vector.quantize_mx(out=codes[:].bitcast(FP8X4), scales=scales[:], in_=woven[w][:].rearrange("p n j -> p (n j)"))
+            for c in range(first, last, P):
+                for bank, (a, b) in zip(banks, spans(BANKS)):
+                    if a <= c < b:
                         nc.tensor.matmul_mx(
                             out=bank[:, c - a : c - a + P],
                             lhsT=codes[:, c - first : c - first + P].bitcast(FP8X4),
@@ -147,11 +159,21 @@ def tile_picked_cbn_silu_e_kernel(tc, xT, w1_words, w1_scales, gamma, beta, offs
                             stop=True,
                         )
 
-        for s, (a, b) in enumerate(parts):
-            scaled = keep.tile([P, b - a], F32, name="scaled%d" % s)
+        scaled = keep.tile([P, S], F32, name="picked%d" % (len(pieces) - 1))
+
+        def finish(s):
+            a, b = parts[s]
             result = keep.tile([P, b - a], F32, name="result%d" % s)
-            nc.vector.tensor_tensor(scaled[:], banks[s][:], gamma_turned[:, a:b], ALU.mult)
+            for bank, (first, last) in zip(banks, spans(BANKS)):
+                lo, hi = max(a, first), min(b, last)
+                if lo < hi:
+                    nc.vector.tensor_tensor(scaled[:, lo:hi], bank[:, lo - first : hi - first], gamma_turned[:, lo:hi], ALU.mult)
             for c in range(a, b, P):
-                nc.tensor.matmul(sums[s][:, c - a : c - a + P], lhsT=scaled[:, c - a : c - a + P], rhs=ident[:], is_transpose=True, start=False, stop=(c + P == b))
+                nc.tensor.matmul(sums[s][:, c - a : c - a + P], lhsT=scaled[:, c : c + P], rhs=ident[:], is_transpose=True, start=False, stop=(c + P == b))
             nc.scalar.activation(result[:], sums[s][:], ACT.Silu, bias=zero_bias[:])
             nc.sync.dma_start(out[:, a:b], result[:])
+
+        for w in range(len(sheets)):
+            quantise(w)
+        for s in range(len(parts)):
+            finish(s)

@@ -23,8 +23,8 @@ PIECES = (256, 256, 256, 256)
 SHEETS = (256, 256, 256, 128, 128)
 BANKS = (384, 512, 128)
 PARTS = (128, 256, 256, 256, 128)
-LOW_CHUNKS = ((1024, 0), (1024, 608))
-HIGH_CHUNKS = ((512, 0), (768, 0), (512, 512), (256, 96))
+LOW_CHUNKS = ((2048, 1312),)
+HIGH_CHUNKS = ((640, 0), (640, 0), (512, 512), (256, 176))
 
 
 def spans(widths):
@@ -117,13 +117,13 @@ def tile_picked_cbn_silu_e_kernel(tc, xT, w1_words, w1_scales, gamma, beta, offs
 
         gamma_turned = keep.tile([P, S], F32, name="gamma_turned")
         turn(gamma_pick[0], gamma_turned[:, :CLASS_PIECE], nc.scalar.copy)
-        turn(gamma_pick[1], gamma_turned[:, CLASS_PIECE:], nc.vector.tensor_copy)
+        turn(gamma_pick[1], gamma_turned[:, CLASS_PIECE:], nc.scalar.copy)
 
-        low = round_pair("gamma_pick0", LOW_CHUNKS, low_raw)
+        beta_turned = [keep.tile([P, CLASS_PIECE], F32, name="beta_turned0")]
+        turn(beta_pick[0], beta_turned[0][:], nc.scalar.copy)
+        low = round_pair("beta_pick0", LOW_CHUNKS, low_raw)
         for i in range(len(pieces)):
             gather_pair(0, low, i)
-        beta_turned = [keep.tile([P, CLASS_PIECE], F32, name="raw0_1")]
-        turn(beta_pick[0], beta_turned[0][:], nc.scalar.copy)
         high = round_pair("high", HIGH_CHUNKS, high_raw)
         beta_turned.append(keep.tile([P, CLASS_PIECE], F32, name="raw1_%d" % (len(HIGH_CHUNKS) - 1)))
         turn(beta_pick[1], beta_turned[1][:], nc.scalar.copy)

@@ -23,8 +23,8 @@ PIECES = (256, 256, 256, 256)
 SHEETS = (256, 256, 256, 128, 128)
 BANKS = (384, 512, 128)
 PARTS = (128, 256, 256, 256, 128)
-LOW_CHUNKS = ((2048, 1312),)
-HIGH_CHUNKS = ((640, 0), (640, 0), (512, 512), (256, 176))
+LOW_CHUNKS = ((2048, 1280, 0),)
+HIGH_CHUNKS = ((768, 0, 320), (640, 0, 256), (384, 0, 128), (256, 160, 0))
 
 
 def spans(widths):
@@ -54,17 +54,17 @@ def tile_picked_cbn_silu_e_kernel(tc, xT, w1_words, w1_scales, gamma, beta, offs
         nc.sync.dma_start(cls_sb[:], cls)
         nc.sync.dma_start(gamma_sb[:], gamma)
         nc.sync.dma_start(beta_sb[:], beta)
-        nc.sync.dma_start(offs_sb[:], offs)
 
         def load_pair(u, chunks):
             tiles = []
-            for c, (a, b) in enumerate(spans([width for width, share in chunks])):
+            for c, (a, b) in enumerate(spans([chunk[0] for chunk in chunks])):
                 raw = keep.tile([P, 2, b - a], F32, name="raw%d_%d" % (u, c))
                 nc.sync.dma_start(raw[:], x_rows[:, 2 * u : 2 * u + 2, a:b])
                 tiles.append(raw)
             return tiles
 
         low_raw = load_pair(0, LOW_CHUNKS)
+        nc.sync.dma_start(offs_sb[:], offs)
         high_raw = load_pair(1, HIGH_CHUNKS)
 
         w_codes = keep.tile([P, 2 * N], U8, name="w_codes", align_bytes=64)
@@ -97,9 +97,11 @@ def tile_picked_cbn_silu_e_kernel(tc, xT, w1_words, w1_scales, gamma, beta, offs
 
         def round_pair(name, chunks, tiles):
             pair = keep.tile([P, T, 2], BF16, name=name)
-            for raw, (width, share), (a, b) in zip(tiles, chunks, spans([width for width, share in chunks])):
-                if share < width:
-                    nc.scalar.copy(pair[:, a + share : b, :], raw[:, :, share:].rearrange("p j t -> p t j"))
+            for raw, (width, share, pool_share), (a, b) in zip(tiles, chunks, spans([chunk[0] for chunk in chunks])):
+                end = width - pool_share
+                if end < width:
+                    nc.gpsimd.tensor_scalar(pair[:, a + end : b, :], raw[:, :, end:].rearrange("p j t -> p t j"), 1.0, 0.0, ALU.mult, ALU.add)
+                nc.scalar.copy(pair[:, a + share : a + end, :], raw[:, :, share:end].rearrange("p j t -> p t j"))
                 if share > 0:
                     nc.vector.tensor_copy(pair[:, a : a + share, :], raw[:, :, :share].rearrange("p j t -> p t j"))
             return pair

@@ -24,7 +24,7 @@ SHEETS = (256, 256, 256, 128, 128)
 BANKS = (384, 512, 128)
 PARTS = (128, 256, 256, 256, 128)
 LOW_CHUNKS = ((2048, 1280, 0),)
-HIGH_CHUNKS = ((768, 0, 320), (640, 0, 256), (384, 0, 128), (256, 160, 0))
+HIGH_CHUNKS = ((1024, 0, 416), (704, 448, 0), (320, 208, 0))
 
 
 def spans(widths):
@@ -52,27 +52,12 @@ def tile_picked_cbn_silu_e_kernel(tc, xT, w1_words, w1_scales, gamma, beta, offs
         beta_sb = keep.tile([P, U], F32, name="beta_sb")
 
         nc.sync.dma_start(cls_sb[:], cls)
-        nc.sync.dma_start(gamma_sb[:], gamma)
-        nc.sync.dma_start(beta_sb[:], beta)
-
-        def load_pair(u, chunks):
-            tiles = []
-            for c, (a, b) in enumerate(spans([chunk[0] for chunk in chunks])):
-                raw = keep.tile([P, 2, b - a], F32, name="raw%d_%d" % (u, c))
-                nc.sync.dma_start(raw[:], x_rows[:, 2 * u : 2 * u + 2, a:b])
-                tiles.append(raw)
-            return tiles
-
-        low_raw = load_pair(0, LOW_CHUNKS)
         nc.sync.dma_start(offs_sb[:], offs)
-        high_raw = load_pair(1, HIGH_CHUNKS)
+        nc.scalar.dma_start(gamma_sb[:], gamma)
+        nc.scalar.dma_start(beta_sb[:], beta)
 
-        w_codes = keep.tile([P, 2 * N], U8, name="w_codes", align_bytes=64)
-        w_scale = keep.tile([P, N], U8, name="w_scale", align_bytes=64)
-        nc.gpsimd.memset(w_scale[:], 0)
-        nc.sync.dma_start(w_codes[:].bitcast(I32), w1_words[0].bitcast(I32))
-        for q in range(4):
-            nc.sync.dma_start(w_scale[32 * q : 32 * q + 4, :].bitcast(I32), w1_scales[0, 4 * q : 4 * q + 4, :].bitcast(I32))
+        low_raw = keep.tile([P, 2, T], F32, name="low_raw", align_bytes=64)
+        nc.scalar.dma_start(low_raw[:], x_rows[:, 0:2, :])
 
         zero_in = keep.tile([P, 1], F32, name="zero_in")
         zero_bias = keep.tile([P, 1], F32, name="zero_bias")
@@ -84,7 +69,7 @@ def tile_picked_cbn_silu_e_kernel(tc, xT, w1_words, w1_scales, gamma, beta, offs
         def look_up(table, name):
             halves = []
             for a in range(0, S, CLASS_PIECE):
-                pick = keep.tile([P, CLASS_PIECE], F32, name="%s%d" % (name, a // CLASS_PIECE))
+                pick = keep.tile([P, CLASS_PIECE], F32, name="%s%d" % (name, a // CLASS_PIECE), align_bytes=64)
                 nc.vector.tensor_copy(pick[:], table[:].indirect(cls_sb[:, a // 16 : (a + CLASS_PIECE) // 16]))
                 halves.append(pick)
             return halves
@@ -96,7 +81,7 @@ def tile_picked_cbn_silu_e_kernel(tc, xT, w1_words, w1_scales, gamma, beta, offs
         woven = [keep.tile([P, b - a, 4], BF16, name="woven%d" % i, align_bytes=64) for i, (a, b) in enumerate(sheets)]
 
         def round_pair(name, chunks, tiles):
-            pair = keep.tile([P, T, 2], BF16, name=name)
+            pair = keep.tile([P, T, 2], BF16, name=name, align_bytes=64)
             for raw, (width, share, pool_share), (a, b) in zip(tiles, chunks, spans([chunk[0] for chunk in chunks])):
                 end = width - pool_share
                 if end < width:
@@ -121,14 +106,26 @@ def tile_picked_cbn_silu_e_kernel(tc, xT, w1_words, w1_scales, gamma, beta, offs
         turn(gamma_pick[0], gamma_turned[:, :CLASS_PIECE], nc.scalar.copy)
         turn(gamma_pick[1], gamma_turned[:, CLASS_PIECE:], nc.scalar.copy)
 
+        high_rows = keep.tile([P, 2, T], F32, name="gamma_pick1", align_bytes=64)
+        high_raw = []
+        for a, b in spans([chunk[0] for chunk in HIGH_CHUNKS]):
+            nc.sync.dma_start(high_rows[:, :, a:b], x_rows[:, 2:4, a:b])
+            high_raw.append(high_rows[:, :, a:b])
+
         beta_turned = [keep.tile([P, CLASS_PIECE], F32, name="beta_turned0")]
         turn(beta_pick[0], beta_turned[0][:], nc.scalar.copy)
-        low = round_pair("beta_pick0", LOW_CHUNKS, low_raw)
+        low = round_pair("beta_pick0", LOW_CHUNKS, [low_raw])
         for i in range(len(pieces)):
             gather_pair(0, low, i)
         high = round_pair("high", HIGH_CHUNKS, high_raw)
-        beta_turned.append(keep.tile([P, CLASS_PIECE], F32, name="raw1_%d" % (len(HIGH_CHUNKS) - 1)))
+        beta_turned.append(keep.tile([P, CLASS_PIECE], F32, name="gamma_pick1", align_bytes=64))
         turn(beta_pick[1], beta_turned[1][:], nc.scalar.copy)
+        w_codes = keep.tile([P, 2 * N], U8, name="low_raw", align_bytes=64)
+        w_scale = keep.tile([P, N], U8, name="beta_pick1", align_bytes=64)
+        nc.gpsimd.memset(w_scale[:], 0)
+        nc.sync.dma_start(w_codes[:].bitcast(I32), w1_words[0].bitcast(I32))
+        for q in range(4):
+            nc.sync.dma_start(w_scale[32 * q : 32 * q + 4, :].bitcast(I32), w1_scales[0, 4 * q : 4 * q + 4, :].bitcast(I32))
         sums = [psum.tile([P, b - a], F32, name="sum%d" % s) for s, (a, b) in enumerate(parts)]
         for s, (a, b) in enumerate(parts):
             for c in range(a, b, P):

@@ -24,7 +24,7 @@ SHEETS = (256, 256, 256, 128, 128)
 BANKS = (384, 512, 128)
 PARTS = (128, 256, 256, 256, 128)
 LOW_CHUNKS = ((2048, 1280, 0),)
-HIGH_CHUNKS = ((1024, 0, 416), (704, 448, 0), (320, 208, 0))
+HIGH_CHUNKS = ((1088, 0, 448), (640, 0, 256), (320, 240, 0))
 
 
 def spans(widths):

@@ -1,7 +1,6 @@
 from contextlib import ExitStack
 
 import concourse.mybir as mybir
-from concourse.masks import make_identity
 
 K, T, S, N, U = 512, 2048, 1024, 128, 1024
 FLOPS = 2 * K * N * S
@@ -18,13 +17,12 @@ ACT = mybir.ActivationFunctionType
 ALU = mybir.AluOpType
 
 P = 128
-CLASS_PIECE = 512
-PIECES = (256, 256, 256, 256)
-SHEETS = (256, 256, 256, 128, 128)
-BANKS = (384, 512, 128)
-PARTS = (128, 256, 256, 256, 128)
-LOW_CHUNKS = ((2048, 1280, 0),)
-HIGH_CHUNKS = ((1088, 0, 448), (640, 0, 256), (320, 240, 0))
+LOW_CHUNKS = ((1024, 640), (1024, 704))
+HIGH_CHUNKS = ((1024, 576), (640, 384), (384, 256))
+HALF = 512
+PIECE = 256
+LAST = 128
+SHIFTS = (256, 256, 256, 128)
 
 
 def spans(widths):
@@ -38,9 +36,7 @@ def spans(widths):
 def tile_picked_cbn_silu_e_kernel(tc, xT, w1_words, w1_scales, gamma, beta, offs, cls, out):
     nc = tc.nc
     x_rows = xT.rearrange("(p j) t -> p j t", j=4)
-    pieces = spans(PIECES)
-    sheets = spans(SHEETS)
-    parts = spans(PARTS)
+    pieces = spans([PIECE] * (S // PIECE))
 
     with ExitStack() as ctx:
         keep = ctx.enter_context(tc.tile_pool(name="keep", bufs=1))
@@ -48,131 +44,106 @@ def tile_picked_cbn_silu_e_kernel(tc, xT, w1_words, w1_scales, gamma, beta, offs
 
         cls_sb = keep.tile([P, S // 16], U16, name="cls_sb")
         offs_sb = keep.tile([P, S // 16], U16, name="offs_sb")
+
+        def load_pair(u, chunks, between):
+            tiles = []
+            for i, (a, b) in enumerate(spans([width for width, share in chunks])):
+                raw = keep.tile([P, 2, b - a], F32, name="raw%d_%d" % (u, i))
+                nc.sync.dma_start(raw[:], x_rows[:, 2 * u : 2 * u + 2, a:b])
+                tiles.append(raw)
+                if i == 0:
+                    nc.sync.dma_start(*between)
+            return tiles
+
+        low_raw = load_pair(0, LOW_CHUNKS, (offs_sb[:], offs))
+        high_raw = load_pair(1, HIGH_CHUNKS, (cls_sb[:], cls))
         gamma_sb = keep.tile([P, U], F32, name="gamma_sb")
         beta_sb = keep.tile([P, U], F32, name="beta_sb")
-
-        nc.sync.dma_start(cls_sb[:], cls)
-        nc.sync.dma_start(offs_sb[:], offs)
-        nc.scalar.dma_start(gamma_sb[:], gamma)
-        nc.scalar.dma_start(beta_sb[:], beta)
-
-        low_raw = keep.tile([P, 2, T], F32, name="low_raw", align_bytes=64)
-        nc.scalar.dma_start(low_raw[:], x_rows[:, 0:2, :])
+        nc.sync.dma_start(gamma_sb[:], gamma)
+        nc.sync.dma_start(beta_sb[:], beta)
 
         zero_in = keep.tile([P, 1], F32, name="zero_in")
         zero_bias = keep.tile([P, 1], F32, name="zero_bias")
         nc.gpsimd.memset(zero_in[:], 0.0)
         nc.scalar.activation(zero_bias[:], zero_in[:], ACT.Silu)
-        ident = keep.tile([P, P], F32, name="ident")
-        make_identity(nc, ident[:])
 
-        def look_up(table, name):
-            halves = []
-            for a in range(0, S, CLASS_PIECE):
-                pick = keep.tile([P, CLASS_PIECE], F32, name="%s%d" % (name, a // CLASS_PIECE), align_bytes=64)
-                nc.vector.tensor_copy(pick[:], table[:].indirect(cls_sb[:, a // 16 : (a + CLASS_PIECE) // 16]))
-                halves.append(pick)
-            return halves
-
-        gamma_pick = look_up(gamma_sb, "gamma_pick")
-        beta_pick = look_up(beta_sb, "beta_pick")
-
-        picked = [keep.tile([P, 2, b - a], U32, name="picked%d" % i) for i, (a, b) in enumerate(pieces)]
-        woven = [keep.tile([P, b - a, 4], BF16, name="woven%d" % i, align_bytes=64) for i, (a, b) in enumerate(sheets)]
-
-        def round_pair(name, chunks, tiles):
-            pair = keep.tile([P, T, 2], BF16, name=name, align_bytes=64)
-            for raw, (width, share, pool_share), (a, b) in zip(tiles, chunks, spans([chunk[0] for chunk in chunks])):
-                end = width - pool_share
-                if end < width:
-                    nc.gpsimd.tensor_scalar(pair[:, a + end : b, :], raw[:, :, end:].rearrange("p j t -> p t j"), 1.0, 0.0, ALU.mult, ALU.add)
-                nc.scalar.copy(pair[:, a + share : a + end, :], raw[:, :, share:end].rearrange("p j t -> p t j"))
-                if share > 0:
-                    nc.vector.tensor_copy(pair[:, a : a + share, :], raw[:, :, :share].rearrange("p j t -> p t j"))
-            return pair
-
-        def gather_pair(u, pair, i):
-            a, b = pieces[i]
-            window = pair[:].rearrange("p t j -> p (t j)").bitcast(U32)
-            nc.vector.tensor_copy(picked[i][:, u, :], window.indirect(offs_sb[:, a // 16 : b // 16]))
-
-        def turn(pick, turned, copy):
-            bank = psum.tile([P, CLASS_PIECE], F32, name="turn_bank", tag="work", bufs=3)
-            for c in range(0, CLASS_PIECE, P):
-                nc.tensor.transpose(bank[:, c : c + P], pick[:, c : c + P], ident[:])
-            copy(turned, bank[:])
-
-        gamma_turned = keep.tile([P, S], F32, name="gamma_turned")
-        turn(gamma_pick[0], gamma_turned[:, :CLASS_PIECE], nc.scalar.copy)
-        turn(gamma_pick[1], gamma_turned[:, CLASS_PIECE:], nc.scalar.copy)
-
-        high_rows = keep.tile([P, 2, T], F32, name="gamma_pick1", align_bytes=64)
-        high_raw = []
-        for a, b in spans([chunk[0] for chunk in HIGH_CHUNKS]):
-            nc.sync.dma_start(high_rows[:, :, a:b], x_rows[:, 2:4, a:b])
-            high_raw.append(high_rows[:, :, a:b])
-
-        beta_turned = [keep.tile([P, CLASS_PIECE], F32, name="beta_turned0")]
-        turn(beta_pick[0], beta_turned[0][:], nc.scalar.copy)
-        low = round_pair("beta_pick0", LOW_CHUNKS, [low_raw])
-        for i in range(len(pieces)):
-            gather_pair(0, low, i)
-        high = round_pair("high", HIGH_CHUNKS, high_raw)
-        beta_turned.append(keep.tile([P, CLASS_PIECE], F32, name="gamma_pick1", align_bytes=64))
-        turn(beta_pick[1], beta_turned[1][:], nc.scalar.copy)
-        w_codes = keep.tile([P, 2 * N], U8, name="low_raw", align_bytes=64)
-        w_scale = keep.tile([P, N], U8, name="beta_pick1", align_bytes=64)
-        nc.gpsimd.memset(w_scale[:], 0)
+        w_codes = keep.tile([P, 2 * N], U8, name="w_codes", align_bytes=64)
+        w_scale = keep.tile([P, N], U8, name="w_scale", align_bytes=64)
+        nc.gpsimd.memset(w_scale[:].bitcast(I32), 0)
         nc.sync.dma_start(w_codes[:].bitcast(I32), w1_words[0].bitcast(I32))
         for q in range(4):
             nc.sync.dma_start(w_scale[32 * q : 32 * q + 4, :].bitcast(I32), w1_scales[0, 4 * q : 4 * q + 4, :].bitcast(I32))
-        sums = [psum.tile([P, b - a], F32, name="sum%d" % s) for s, (a, b) in enumerate(parts)]
-        for s, (a, b) in enumerate(parts):
-            for c in range(a, b, P):
-                half, at = divmod(c, CLASS_PIECE)
-                nc.tensor.matmul(sums[s][:, c - a : c - a + P], lhsT=beta_turned[half][:, at : at + P], rhs=ident[:], is_transpose=True, start=(c == a), stop=False)
+
+        def entries(tile, a, b):
+            return tile[:, a // 16 : b // 16]
+
+        def round_pair(name, chunks, tiles):
+            pair = keep.tile([P, T, 2], BF16, name=name, align_bytes=64)
+            for raw, (width, share), (a, b) in zip(tiles, chunks, spans([chunk[0] for chunk in chunks])):
+                nc.scalar.copy(pair[:, a + share : b, :], raw[:, :, share:].rearrange("p j t -> p t j"))
+                nc.vector.tensor_copy(pair[:, a : a + share, :], raw[:, :, :share].rearrange("p j t -> p t j"))
+            return pair[:].rearrange("p t j -> p (t j)").bitcast(U32)
+
+        picked = [keep.tile([P, 2, PIECE], U32, name="picked%d" % i) for i in range(len(pieces))]
+        low = round_pair("low", LOW_CHUNKS, low_raw)
+        for i, (a, b) in enumerate(pieces):
+            nc.vector.tensor_copy(picked[i][:, 0, :], low.indirect(entries(offs_sb, a, b)))
+        high = round_pair("high", HIGH_CHUNKS, high_raw)
+        for i, (a, b) in enumerate(pieces):
+            nc.vector.tensor_copy(picked[i][:, 1, :], high.indirect(entries(offs_sb, a, b)))
+
+        woven = []
         for i in range(len(pieces)):
-            gather_pair(1, high, i)
-            first, last = pieces[i]
-            for w, (a, b) in enumerate(sheets):
-                if first <= a < last:
-                    words = woven[w][:].rearrange("p n j -> p (n j)").bitcast(U32).rearrange("p (n u) -> p n u", u=2)
-                    nc.scalar.copy(words, picked[i][:, :, a - first : b - first].rearrange("p u n -> p n u"))
+            sheet = keep.tile([P, PIECE, 4], BF16, name="woven%d" % i, align_bytes=64)
+            words = sheet[:].rearrange("p n j -> p (n j)").bitcast(U32).rearrange("p (n u) -> p n u", u=2)
+            source = picked[i][:].rearrange("p u n -> p n u")
+            if i < len(pieces) - 1:
+                nc.gpsimd.tensor_copy(words, source)
+            else:
+                nc.vector.tensor_copy(words.bitcast(I32), source.bitcast(I32))
+            woven.append(sheet)
 
-        banks = [psum.tile([P, b - a], F32, name="mx_bank", tag="work", bufs=3) for a, b in spans(BANKS)]
-        def quantise(w):
-            first, last = sheets[w]
-            codes = keep.tile([P, last - first], U32, name="codes%d" % w, align_bytes=64)
-            scales = keep.tile([P, last - first], U8, name="scales%d" % w, align_bytes=64)
-            nc.vector.quantize_mx(out=codes[:].bitcast(FP8X4), scales=scales[:], in_=woven[w][:].rearrange("p n j -> p (n j)"))
-            for c in range(first, last, P):
-                for bank, (a, b) in zip(banks, spans(BANKS)):
-                    if a <= c < b:
-                        nc.tensor.matmul_mx(
-                            out=bank[:, c - a : c - a + P],
-                            lhsT=codes[:, c - first : c - first + P].bitcast(FP8X4),
-                            lhsT_scale=scales[:, c - first : c - first + P],
-                            rhs=w_codes[:].bitcast(FP4X4),
-                            rhs_scale=w_scale[:],
-                            start=True,
-                            stop=True,
-                        )
+        def pick_table(table, name, a, b):
+            pick = keep.tile([P, b - a], F32, name=name)
+            nc.scalar.activation(pick[:], table[:].indirect(entries(cls_sb, a, b)), ACT.Copy)
+            return pick
 
-        scaled = keep.tile([P, S], F32, name="picked%d" % (len(pieces) - 1))
+        gains = [pick_table(gamma_sb, "gains%d" % h, h * HALF, (h + 1) * HALF) for h in range(2)]
+        shifts = [pick_table(beta_sb, "shifts%d" % i, a, b) for i, (a, b) in enumerate(spans(SHIFTS))]
 
-        def finish(s):
-            a, b = parts[s]
-            result = keep.tile([P, b - a], F32, name="result%d" % s)
-            for bank, (first, last) in zip(banks, spans(BANKS)):
-                lo, hi = max(a, first), min(b, last)
-                if lo < hi:
-                    nc.vector.tensor_tensor(scaled[:, lo:hi], bank[:, lo - first : hi - first], gamma_turned[:, lo:hi], ALU.mult)
-            for c in range(a, b, P):
-                nc.tensor.matmul(sums[s][:, c - a : c - a + P], lhsT=scaled[:, c : c + P], rhs=ident[:], is_transpose=True, start=False, stop=(c + P == b))
-            nc.scalar.activation(result[:], sums[s][:], ACT.Silu, bias=zero_bias[:])
+        banks = []
+        for i in range(len(pieces)):
+            codes = keep.tile([P, PIECE], U32, name="codes%d" % i, align_bytes=64)
+            scales = keep.tile([P, PIECE], U8, name="scales%d" % i, align_bytes=64)
+            nc.vector.quantize_mx(out=codes[:].bitcast(FP8X4), scales=scales[:], in_=woven[i][:].rearrange("p n j -> p (n j)"))
+            bank = psum.tile([P, PIECE], F32, name="bank%d" % i)
+            nc.tensor.matmul_mx(
+                out=bank[:],
+                lhsT=w_codes[:].bitcast(FP4X4),
+                lhsT_scale=w_scale[:],
+                rhs=codes[:].bitcast(FP8X4),
+                rhs_scale=scales[:],
+                start=True,
+                stop=True,
+            )
+            banks.append(bank)
+
+        scaled = []
+        for i, (a, b) in enumerate(pieces):
+            product = keep.tile([P, PIECE], F32, name="scaled%d" % i)
+            nc.vector.tensor_tensor(product[:], banks[i][:], gains[a // HALF][:, a % HALF : a % HALF + PIECE], ALU.mult)
+            scaled.append(product)
+
+        def finish(shifted, a, b):
+            result = keep.tile([P, b - a], F32, name="result%d" % a)
+            nc.scalar.activation(result[:], shifted[:], ACT.Silu, bias=zero_bias[:])
             nc.sync.dma_start(out[:, a:b], result[:])
 
-        for w in range(len(sheets)):
-            quantise(w)
-        for s in range(len(parts)):
-            finish(s)
+        for i, (a, b) in enumerate(spans(SHIFTS)):
+            shifted = keep.tile([P, b - a], F32, name="shifted%d" % a)
+            engine = nc.gpsimd if i < 2 else nc.vector
+            engine.tensor_tensor(shifted[:], scaled[i][:, : b - a], shifts[i][:], ALU.add)
+            finish(shifted, a, b)
+        shifted = keep.tile([P, LAST], F32, name="shifted_last")
+        nc.vector.tensor_tensor(shifted[:], beta_sb[:].indirect(entries(cls_sb, S - LAST, S)), scaled[-1][:, PIECE - LAST :], ALU.add)
+        finish(shifted, S - LAST, S)

@@ -17,12 +17,13 @@ ACT = mybir.ActivationFunctionType
 ALU = mybir.AluOpType
 
 P = 128
-LOW_CHUNKS = ((1024, 640), (1024, 704))
-HIGH_CHUNKS = ((1024, 576), (640, 384), (384, 256))
+LOW_CHUNKS = ((2048, 1344, 0),)
+HIGH_CHUNKS = ((1024, 0, 416), (640, 0, 256), (384, 256, 0))
 HALF = 512
+OVERRUN = 16
 PIECE = 256
-LAST = 128
-SHIFTS = (256, 256, 256, 128)
+PARTS = (256, 256, 256, 128, 128)
+POOL_PARTS = 1
 
 
 def spans(widths):
@@ -33,10 +34,15 @@ def spans(widths):
     return result
 
 
+def places(chunks):
+    return [(T - b, T - a) for a, b in spans([chunk[0] for chunk in chunks])]
+
+
 def tile_picked_cbn_silu_e_kernel(tc, xT, w1_words, w1_scales, gamma, beta, offs, cls, out):
     nc = tc.nc
     x_rows = xT.rearrange("(p j) t -> p j t", j=4)
     pieces = spans([PIECE] * (S // PIECE))
+    halves = spans([HALF] * (S // HALF))
 
     with ExitStack() as ctx:
         keep = ctx.enter_context(tc.tile_pool(name="keep", bufs=1))
@@ -44,72 +50,80 @@ def tile_picked_cbn_silu_e_kernel(tc, xT, w1_words, w1_scales, gamma, beta, offs
 
         cls_sb = keep.tile([P, S // 16], U16, name="cls_sb")
         offs_sb = keep.tile([P, S // 16], U16, name="offs_sb")
+        nc.sync.dma_start(offs_sb[:], offs)
+        nc.sync.dma_start(cls_sb[:], cls)
 
-        def load_pair(u, chunks, between):
+        def load_pair(u, chunks):
             tiles = []
-            for i, (a, b) in enumerate(spans([width for width, share in chunks])):
-                raw = keep.tile([P, 2, b - a], F32, name="raw%d_%d" % (u, i))
-                nc.sync.dma_start(raw[:], x_rows[:, 2 * u : 2 * u + 2, a:b])
+            for i, (a, b) in enumerate(places(chunks)):
+                raw = keep.tile([P, 2, b - a], F32, name="raw%d_%d" % (u, i), align_bytes=64)
+                nc.scalar.dma_start(raw[:], x_rows[:, 2 * u : 2 * u + 2, a:b])
                 tiles.append(raw)
-                if i == 0:
-                    nc.sync.dma_start(*between)
             return tiles
 
-        low_raw = load_pair(0, LOW_CHUNKS, (offs_sb[:], offs))
-        high_raw = load_pair(1, HIGH_CHUNKS, (cls_sb[:], cls))
+        low_raw = load_pair(0, LOW_CHUNKS)
+        high_raw = load_pair(1, HIGH_CHUNKS)
         gamma_sb = keep.tile([P, U], F32, name="gamma_sb")
         beta_sb = keep.tile([P, U], F32, name="beta_sb")
-        nc.sync.dma_start(gamma_sb[:], gamma)
-        nc.sync.dma_start(beta_sb[:], beta)
+        nc.scalar.dma_start(gamma_sb[:], gamma)
+        nc.scalar.dma_start(beta_sb[:], beta)
 
         zero_in = keep.tile([P, 1], F32, name="zero_in")
         zero_bias = keep.tile([P, 1], F32, name="zero_bias")
         nc.gpsimd.memset(zero_in[:], 0.0)
         nc.scalar.activation(zero_bias[:], zero_in[:], ACT.Silu)
 
-        w_codes = keep.tile([P, 2 * N], U8, name="w_codes", align_bytes=64)
-        w_scale = keep.tile([P, N], U8, name="w_scale", align_bytes=64)
+        def entries(tile, a, b):
+            return tile[:, a // 16 : b // 16]
+
+        pairs = keep.tile([P, 2 * T, 2], BF16, name="pairs", align_bytes=64)
+        pair_words = pairs[:].rearrange("p t j -> p (t j)").bitcast(U32)
+
+        def round_pair(u, chunks, tiles):
+            pair = pairs[:, u * T : (u + 1) * T, :]
+            for raw, (width, share, pool_share), (a, b) in zip(tiles, chunks, places(chunks)):
+                end = width - pool_share
+                if end < width:
+                    nc.gpsimd.tensor_scalar(pair[:, a + end : b, :], raw[:, :, end:].rearrange("p j t -> p t j"), 1.0, 0.0, ALU.mult, ALU.add)
+                nc.scalar.copy(pair[:, a + share : a + end, :], raw[:, :, share:end].rearrange("p j t -> p t j"))
+                if share > 0:
+                    nc.vector.tensor_copy(pair[:, a : a + share, :], raw[:, :, :share].rearrange("p j t -> p t j"))
+
+        picked = keep.tile([P, 2, S], U32, name="picked")
+        round_pair(0, LOW_CHUNKS, low_raw)
+        for a, b in halves:
+            window = pair_words[:, : T + OVERRUN] if b == S else pair_words[:, :T]
+            nc.vector.tensor_copy(picked[:, 0, a:b], window.indirect(entries(offs_sb, a, b)))
+        round_pair(1, HIGH_CHUNKS, high_raw)
+        for a, b in pieces:
+            nc.vector.tensor_copy(picked[:, 1, a:b], pair_words[:, T:].indirect(entries(offs_sb, a, b)))
+
+        w_codes = keep.tile([P, 2 * N], U8, name="raw0_0", align_bytes=64)
+        w_scale = keep.tile([P, N], U8, name="raw1_0", align_bytes=64)
         nc.gpsimd.memset(w_scale[:].bitcast(I32), 0)
         nc.sync.dma_start(w_codes[:].bitcast(I32), w1_words[0].bitcast(I32))
         for q in range(4):
             nc.sync.dma_start(w_scale[32 * q : 32 * q + 4, :].bitcast(I32), w1_scales[0, 4 * q : 4 * q + 4, :].bitcast(I32))
 
-        def entries(tile, a, b):
-            return tile[:, a // 16 : b // 16]
-
-        def round_pair(name, chunks, tiles):
-            pair = keep.tile([P, T, 2], BF16, name=name, align_bytes=64)
-            for raw, (width, share), (a, b) in zip(tiles, chunks, spans([chunk[0] for chunk in chunks])):
-                nc.scalar.copy(pair[:, a + share : b, :], raw[:, :, share:].rearrange("p j t -> p t j"))
-                nc.vector.tensor_copy(pair[:, a : a + share, :], raw[:, :, :share].rearrange("p j t -> p t j"))
-            return pair[:].rearrange("p t j -> p (t j)").bitcast(U32)
-
-        picked = [keep.tile([P, 2, PIECE], U32, name="picked%d" % i) for i in range(len(pieces))]
-        low = round_pair("low", LOW_CHUNKS, low_raw)
-        for i, (a, b) in enumerate(pieces):
-            nc.vector.tensor_copy(picked[i][:, 0, :], low.indirect(entries(offs_sb, a, b)))
-        high = round_pair("high", HIGH_CHUNKS, high_raw)
-        for i, (a, b) in enumerate(pieces):
-            nc.vector.tensor_copy(picked[i][:, 1, :], high.indirect(entries(offs_sb, a, b)))
-
         woven = []
-        for i in range(len(pieces)):
+        for i, (a, b) in enumerate(pieces):
             sheet = keep.tile([P, PIECE, 4], BF16, name="woven%d" % i, align_bytes=64)
-            words = sheet[:].rearrange("p n j -> p (n j)").bitcast(U32).rearrange("p (n u) -> p n u", u=2)
-            source = picked[i][:].rearrange("p u n -> p n u")
-            if i < len(pieces) - 1:
-                nc.gpsimd.tensor_copy(words, source)
+            if i == 0:
+                values = picked[:, :, a:b].bitcast(BF16).rearrange("p u (n e) -> p n u e", e=2)
+                nc.gpsimd.tensor_scalar(sheet[:].rearrange("p n (u e) -> p n u e", e=2), values, 1.0, 0.0, ALU.mult, ALU.add)
             else:
-                nc.vector.tensor_copy(words.bitcast(I32), source.bitcast(I32))
+                words = sheet[:].rearrange("p n j -> p (n j)").bitcast(I32).rearrange("p (n u) -> p n u", u=2)
+                nc.vector.tensor_copy(words, picked[:, :, a:b].bitcast(I32).rearrange("p u n -> p n u"))
             woven.append(sheet)
 
-        def pick_table(table, name, a, b):
-            pick = keep.tile([P, b - a], F32, name=name)
-            nc.scalar.activation(pick[:], table[:].indirect(entries(cls_sb, a, b)), ACT.Copy)
+        def pick_table(table, name, widths):
+            pick = keep.tile([P, S], F32, name=name)
+            for a, b in widths:
+                nc.scalar.activation(pick[:, a:b], table[:].indirect(entries(cls_sb, a, b)), ACT.Copy)
             return pick
 
-        gains = [pick_table(gamma_sb, "gains%d" % h, h * HALF, (h + 1) * HALF) for h in range(2)]
-        shifts = [pick_table(beta_sb, "shifts%d" % i, a, b) for i, (a, b) in enumerate(spans(SHIFTS))]
+        gains = pick_table(gamma_sb, "gains", halves)
+        shifts = pick_table(beta_sb, "shifts", pieces[:-1])
 
         banks = []
         for i in range(len(pieces)):
@@ -128,22 +142,17 @@ def tile_picked_cbn_silu_e_kernel(tc, xT, w1_words, w1_scales, gamma, beta, offs
             )
             banks.append(bank)
 
-        scaled = []
+        scaled = keep.tile([P, S], F32, name="picked")
         for i, (a, b) in enumerate(pieces):
-            product = keep.tile([P, PIECE], F32, name="scaled%d" % i)
-            nc.vector.tensor_tensor(product[:], banks[i][:], gains[a // HALF][:, a % HALF : a % HALF + PIECE], ALU.mult)
-            scaled.append(product)
+            nc.vector.tensor_tensor(scaled[:, a:b], banks[i][:], gains[:, a:b], ALU.mult)
 
-        def finish(shifted, a, b):
-            result = keep.tile([P, b - a], F32, name="result%d" % a)
+        for s, (a, b) in enumerate(spans(PARTS)):
+            shifted = keep.tile([P, b - a], F32, name="shifted%d" % s)
+            result = keep.tile([P, b - a], F32, name="result%d" % s)
+            if a >= S - PIECE:
+                nc.vector.tensor_tensor(shifted[:], beta_sb[:].indirect(entries(cls_sb, a, b)), scaled[:, a:b], ALU.add)
+            else:
+                engine = nc.gpsimd if s < POOL_PARTS else nc.vector
+                engine.tensor_tensor(shifted[:], scaled[:, a:b], shifts[:, a:b], ALU.add)
             nc.scalar.activation(result[:], shifted[:], ACT.Silu, bias=zero_bias[:])
             nc.sync.dma_start(out[:, a:b], result[:])
-
-        for i, (a, b) in enumerate(spans(SHIFTS)):
-            shifted = keep.tile([P, b - a], F32, name="shifted%d" % a)
-            engine = nc.gpsimd if i < 2 else nc.vector
-            engine.tensor_tensor(shifted[:], scaled[i][:, : b - a], shifts[i][:], ALU.add)
-            finish(shifted, a, b)
-        shifted = keep.tile([P, LAST], F32, name="shifted_last")
-        nc.vector.tensor_tensor(shifted[:], beta_sb[:].indirect(entries(cls_sb, S - LAST, S)), scaled[-1][:, PIECE - LAST :], ALU.add)
-        finish(shifted, S - LAST, S)

@@ -22,8 +22,7 @@ HIGH_CHUNKS = ((1024, 0, 416), (640, 0, 256), (384, 256, 0))
 HALF = 512
 OVERRUN = 16
 PIECE = 256
-PARTS = (256, 256, 256, 128, 128)
-POOL_PARTS = 1
+LAST = 128
 
 
 def spans(widths):
@@ -63,7 +62,7 @@ def tile_picked_cbn_silu_e_kernel(tc, xT, w1_words, w1_scales, gamma, beta, offs
 
         low_raw = load_pair(0, LOW_CHUNKS)
         high_raw = load_pair(1, HIGH_CHUNKS)
-        gamma_sb = keep.tile([P, U], F32, name="gamma_sb")
+        gamma_sb = keep.tile([P, U], F32, name="gamma_sb", align_bytes=64)
         beta_sb = keep.tile([P, U], F32, name="beta_sb")
         nc.scalar.dma_start(gamma_sb[:], gamma)
         nc.scalar.dma_start(beta_sb[:], beta)
@@ -98,23 +97,12 @@ def tile_picked_cbn_silu_e_kernel(tc, xT, w1_words, w1_scales, gamma, beta, offs
         for a, b in pieces:
             nc.vector.tensor_copy(picked[:, 1, a:b], pair_words[:, T:].indirect(entries(offs_sb, a, b)))
 
-        w_codes = keep.tile([P, 2 * N], U8, name="raw0_0", align_bytes=64)
-        w_scale = keep.tile([P, N], U8, name="raw1_0", align_bytes=64)
+        w_codes = keep.tile([P, 2 * N], U8, name="raw1_2", align_bytes=64)
+        w_scale = keep.tile([P, N], U8, name="raw1_1", align_bytes=64)
         nc.gpsimd.memset(w_scale[:].bitcast(I32), 0)
         nc.sync.dma_start(w_codes[:].bitcast(I32), w1_words[0].bitcast(I32))
         for q in range(4):
             nc.sync.dma_start(w_scale[32 * q : 32 * q + 4, :].bitcast(I32), w1_scales[0, 4 * q : 4 * q + 4, :].bitcast(I32))
-
-        woven = []
-        for i, (a, b) in enumerate(pieces):
-            sheet = keep.tile([P, PIECE, 4], BF16, name="woven%d" % i, align_bytes=64)
-            if i == 0:
-                values = picked[:, :, a:b].bitcast(BF16).rearrange("p u (n e) -> p n u e", e=2)
-                nc.gpsimd.tensor_scalar(sheet[:].rearrange("p n (u e) -> p n u e", e=2), values, 1.0, 0.0, ALU.mult, ALU.add)
-            else:
-                words = sheet[:].rearrange("p n j -> p (n j)").bitcast(I32).rearrange("p (n u) -> p n u", u=2)
-                nc.vector.tensor_copy(words, picked[:, :, a:b].bitcast(I32).rearrange("p u n -> p n u"))
-            woven.append(sheet)
 
         def pick_table(table, name, widths):
             pick = keep.tile([P, S], F32, name=name)
@@ -123,10 +111,26 @@ def tile_picked_cbn_silu_e_kernel(tc, xT, w1_words, w1_scales, gamma, beta, offs
             return pick
 
         gains = pick_table(gamma_sb, "gains", halves)
-        shifts = pick_table(beta_sb, "shifts", pieces[:-1])
 
-        banks = []
-        for i in range(len(pieces)):
+        woven = []
+        for i, (a, b) in enumerate(pieces):
+            sheet = keep.tile([P, PIECE, 4], BF16, name="gamma_sb" if b == S else "woven%d" % i, align_bytes=64)
+            words = sheet[:].rearrange("p n j -> p (n j)").bitcast(U32).rearrange("p (n u) -> p n u", u=2)
+            source = picked[:, :, a:b].rearrange("p u n -> p n u")
+            if a == 0:
+                values = picked[:, :, a:b].bitcast(BF16).rearrange("p u (n e) -> p n u e", e=2)
+                nc.gpsimd.tensor_scalar(sheet[:].rearrange("p n (u e) -> p n u e", e=2), values, 1.0, 0.0, ALU.mult, ALU.add)
+            elif b == S:
+                nc.scalar.copy(words, source)
+            else:
+                nc.vector.tensor_copy(words.bitcast(I32), source.bitcast(I32))
+            woven.append(sheet)
+
+        parts = [pieces[1], pieces[2], pieces[0], (S - PIECE, S - LAST), (S - LAST, S)]
+        shifts = pick_table(beta_sb, "shifts", parts[:-1])
+        scaled = keep.tile([P, S], F32, name="picked")
+
+        def multiply(i):
             codes = keep.tile([P, PIECE], U32, name="codes%d" % i, align_bytes=64)
             scales = keep.tile([P, PIECE], U8, name="scales%d" % i, align_bytes=64)
             nc.vector.quantize_mx(out=codes[:].bitcast(FP8X4), scales=scales[:], in_=woven[i][:].rearrange("p n j -> p (n j)"))
@@ -140,19 +144,26 @@ def tile_picked_cbn_silu_e_kernel(tc, xT, w1_words, w1_scales, gamma, beta, offs
                 start=True,
                 stop=True,
             )
-            banks.append(bank)
+            return bank
 
-        scaled = keep.tile([P, S], F32, name="picked")
-        for i, (a, b) in enumerate(pieces):
-            nc.vector.tensor_tensor(scaled[:, a:b], banks[i][:], gains[:, a:b], ALU.mult)
+        def scale(i, bank):
+            a, b = pieces[i]
+            nc.vector.tensor_tensor(scaled[:, a:b], bank[:], gains[:, a:b], ALU.mult)
 
-        for s, (a, b) in enumerate(spans(PARTS)):
-            shifted = keep.tile([P, b - a], F32, name="shifted%d" % s)
+        banks = {i: multiply(i) for i in (1, 2)}
+        scale(1, banks[1])
+        for i in (0, 3):
+            banks[i] = multiply(i)
+        for i in (2, 0, 3):
+            scale(i, banks[i])
+
+        for s, (a, b) in enumerate(parts):
+            shifted = keep.tile([P, b - a], F32, name="gamma_sb" if s == 0 else "shifted%d" % s, align_bytes=64)
             result = keep.tile([P, b - a], F32, name="result%d" % s)
-            if a >= S - PIECE:
+            if b == S:
                 nc.vector.tensor_tensor(shifted[:], beta_sb[:].indirect(entries(cls_sb, a, b)), scaled[:, a:b], ALU.add)
             else:
-                engine = nc.gpsimd if s < POOL_PARTS else nc.vector
+                engine = nc.gpsimd if s == 0 else nc.vector
                 engine.tensor_tensor(shifted[:], scaled[:, a:b], shifts[:, a:b], ALU.add)
             nc.scalar.activation(result[:], shifted[:], ACT.Silu, bias=zero_bias[:])
             nc.sync.dma_start(out[:, a:b], result[:])

@@ -17,92 +17,71 @@ ACT = mybir.ActivationFunctionType
 ALU = mybir.AluOpType
 
 P = 128
-LOW_CHUNKS = ((2048, 1344, 0),)
-HIGH_CHUNKS = ((1024, 0, 416), (640, 0, 256), (384, 256, 0))
 HALF = 512
-OVERRUN = 16
 PIECE = 256
 LAST = 128
-
-
-def spans(widths):
-    result, start = [], 0
-    for width in widths:
-        result.append((start, start + width))
-        start = start + width
-    return result
-
-
-def places(chunks):
-    return [(T - b, T - a) for a, b in spans([chunk[0] for chunk in chunks])]
 
 
 def tile_picked_cbn_silu_e_kernel(tc, xT, w1_words, w1_scales, gamma, beta, offs, cls, out):
     nc = tc.nc
     x_rows = xT.rearrange("(p j) t -> p j t", j=4)
-    pieces = spans([PIECE] * (S // PIECE))
-    halves = spans([HALF] * (S // HALF))
+    pieces = [(a, a + PIECE) for a in range(0, S, PIECE)]
+    halves = [(a, a + HALF) for a in range(0, S, HALF)]
 
     with ExitStack() as ctx:
         keep = ctx.enter_context(tc.tile_pool(name="keep", bufs=1))
+        reuse = ctx.enter_context(tc.tile_pool(name="reuse", bufs=1))
         psum = ctx.enter_context(tc.psum_pool(name="psum", bufs=1))
 
         cls_sb = keep.tile([P, S // 16], U16, name="cls_sb")
         offs_sb = keep.tile([P, S // 16], U16, name="offs_sb")
+        w_codes = keep.tile([P, 2 * N], U8, name="w_codes", align_bytes=64)
+        w_stage = keep.tile([4, 4, N // 4], I32, name="w_stage")
+        w_scale = keep.tile([P, N], U8, name="w_scale", align_bytes=64)
+        nc.sync.dma_start(w_stage[:], w1_scales[0].bitcast(I32).rearrange("(q r) c -> r q c", r=4))
         nc.sync.dma_start(offs_sb[:], offs)
         nc.sync.dma_start(cls_sb[:], cls)
+        nc.sync.dma_start(w_codes[:].bitcast(I32), w1_words[0].bitcast(I32))
 
-        def load_pair(u, chunks):
-            tiles = []
-            for i, (a, b) in enumerate(places(chunks)):
-                raw = keep.tile([P, 2, b - a], F32, name="raw%d_%d" % (u, i), align_bytes=64)
-                nc.scalar.dma_start(raw[:], x_rows[:, 2 * u : 2 * u + 2, a:b])
-                tiles.append(raw)
-            return tiles
-
-        low_raw = load_pair(0, LOW_CHUNKS)
-        high_raw = load_pair(1, HIGH_CHUNKS)
-        gamma_sb = keep.tile([P, U], F32, name="gamma_sb", align_bytes=64)
-        beta_sb = keep.tile([P, U], F32, name="beta_sb")
-        nc.scalar.dma_start(gamma_sb[:], gamma)
-        nc.scalar.dma_start(beta_sb[:], beta)
-
+        rows = []
+        for j in range(4):
+            row = keep.tile([P, T], F32, name="row%d" % j)
+            nc.scalar.dma_start(row[:], x_rows[:, j, :])
+            rows.append(row)
         zero_in = keep.tile([P, 1], F32, name="zero_in")
         zero_bias = keep.tile([P, 1], F32, name="zero_bias")
         nc.gpsimd.memset(zero_in[:], 0.0)
         nc.scalar.activation(zero_bias[:], zero_in[:], ACT.Silu)
 
+        gamma_sb = keep.tile([P, U], F32, name="gamma_sb")
+        beta_sb = keep.tile([P, U], F32, name="beta_sb")
+        nc.scalar.dma_start(gamma_sb[:], gamma)
+        nc.scalar.dma_start(beta_sb[:], beta)
+
+        nc.gpsimd.memset(w_scale[:].bitcast(I32), 0)
+        for q in range(4):
+            nc.vector.tensor_copy(w_scale[32 * q : 32 * q + 4, :].bitcast(I32), w_stage[:, q, :])
+
         def entries(tile, a, b):
             return tile[:, a // 16 : b // 16]
 
-        pairs = keep.tile([P, 2 * T, 2], BF16, name="pairs", align_bytes=64)
-        pair_words = pairs[:].rearrange("p t j -> p (t j)").bitcast(U32)
+        sheets = [keep.tile([P, PIECE, 4], BF16, name="sheet%d" % i, align_bytes=64) for i in range(len(pieces))]
 
-        def round_pair(u, chunks, tiles):
-            pair = pairs[:, u * T : (u + 1) * T, :]
-            for raw, (width, share, pool_share), (a, b) in zip(tiles, chunks, places(chunks)):
-                end = width - pool_share
-                if end < width:
-                    nc.gpsimd.tensor_scalar(pair[:, a + end : b, :], raw[:, :, end:].rearrange("p j t -> p t j"), 1.0, 0.0, ALU.mult, ALU.add)
-                nc.scalar.copy(pair[:, a + share : a + end, :], raw[:, :, share:end].rearrange("p j t -> p t j"))
-                if share > 0:
-                    nc.vector.tensor_copy(pair[:, a : a + share, :], raw[:, :, :share].rearrange("p j t -> p t j"))
-
-        picked = keep.tile([P, 2, S], U32, name="picked")
-        round_pair(0, LOW_CHUNKS, low_raw)
-        for a, b in halves:
-            window = pair_words[:, : T + OVERRUN] if b == S else pair_words[:, :T]
-            nc.vector.tensor_copy(picked[:, 0, a:b], window.indirect(entries(offs_sb, a, b)))
-        round_pair(1, HIGH_CHUNKS, high_raw)
-        for a, b in pieces:
-            nc.vector.tensor_copy(picked[:, 1, a:b], pair_words[:, T:].indirect(entries(offs_sb, a, b)))
-
-        w_codes = keep.tile([P, 2 * N], U8, name="raw1_2", align_bytes=64)
-        w_scale = keep.tile([P, N], U8, name="raw1_1", align_bytes=64)
-        nc.gpsimd.memset(w_scale[:].bitcast(I32), 0)
-        nc.sync.dma_start(w_codes[:].bitcast(I32), w1_words[0].bitcast(I32))
-        for q in range(4):
-            nc.sync.dma_start(w_scale[32 * q : 32 * q + 4, :].bitcast(I32), w1_scales[0, 4 * q : 4 * q + 4, :].bitcast(I32))
+        for u in range(2):
+            dense = reuse.tile([P, 2, PIECE], BF16, name="dense%d" % u, align_bytes=64, offset=(1 - u) * 4 * PIECE)
+            early = keep.tile([P, 2, HALF], BF16, name="early") if u == 0 else None
+            for e in range(2):
+                j = 2 * u + e
+                nc.scalar.activation(dense[:, e, :], rows[j][:].indirect(entries(offs_sb, *pieces[2])), ACT.Copy)
+                if u == 0:
+                    nc.vector.tensor_copy(early[:, e, :], rows[j][:].indirect(entries(offs_sb, *halves[0])))
+                for i in ((3,), (3,), (3, 0, 1), (0, 1, 3))[j]:
+                    nc.vector.tensor_copy(sheets[i][:, :, j], rows[j][:].indirect(entries(offs_sb, *pieces[i])))
+            nc.gpsimd.tensor_scalar(sheets[2][:, :, 2 * u : 2 * u + 2], dense[:].rearrange("p e n -> p n e"), 1.0, 0.0, ALU.mult, ALU.add)
+            if u == 0:
+                for i in (0, 1):
+                    a, b = pieces[i]
+                    nc.scalar.copy(sheets[i][:, :, 0:2], early[:, :, a:b].rearrange("p e n -> p n e"))
 
         def pick_table(table, name, widths):
             pick = keep.tile([P, S], F32, name=name)
@@ -111,29 +90,14 @@ def tile_picked_cbn_silu_e_kernel(tc, xT, w1_words, w1_scales, gamma, beta, offs
             return pick
 
         gains = pick_table(gamma_sb, "gains", halves)
-
-        woven = []
-        for i, (a, b) in enumerate(pieces):
-            sheet = keep.tile([P, PIECE, 4], BF16, name="gamma_sb" if b == S else "woven%d" % i, align_bytes=64)
-            words = sheet[:].rearrange("p n j -> p (n j)").bitcast(U32).rearrange("p (n u) -> p n u", u=2)
-            source = picked[:, :, a:b].rearrange("p u n -> p n u")
-            if a == 0:
-                values = picked[:, :, a:b].bitcast(BF16).rearrange("p u (n e) -> p n u e", e=2)
-                nc.gpsimd.tensor_scalar(sheet[:].rearrange("p n (u e) -> p n u e", e=2), values, 1.0, 0.0, ALU.mult, ALU.add)
-            elif b == S:
-                nc.scalar.copy(words, source)
-            else:
-                nc.vector.tensor_copy(words.bitcast(I32), source.bitcast(I32))
-            woven.append(sheet)
-
-        parts = [pieces[1], pieces[2], pieces[0], (S - PIECE, S - LAST), (S - LAST, S)]
-        shifts = pick_table(beta_sb, "shifts", parts[:-1])
-        scaled = keep.tile([P, S], F32, name="picked")
+        parts = [pieces[0], pieces[3], pieces[1], (HALF, HALF + LAST), (HALF + LAST, S - PIECE)]
+        shifts = pick_table(beta_sb, "shifts", pieces[:3])
+        scaled = keep.tile([P, S], F32, name="scaled")
 
         def multiply(i):
             codes = keep.tile([P, PIECE], U32, name="codes%d" % i, align_bytes=64)
-            scales = keep.tile([P, PIECE], U8, name="scales%d" % i, align_bytes=64)
-            nc.vector.quantize_mx(out=codes[:].bitcast(FP8X4), scales=scales[:], in_=woven[i][:].rearrange("p n j -> p (n j)"))
+            scales = reuse.tile([P, PIECE], U8, name="scales%d" % i, align_bytes=64, offset=i * PIECE)
+            nc.vector.quantize_mx(out=codes[:].bitcast(FP8X4), scales=scales[:], in_=sheets[i][:].rearrange("p n j -> p (n j)"))
             bank = psum.tile([P, PIECE], F32, name="bank%d" % i)
             nc.tensor.matmul_mx(
                 out=bank[:],
@@ -146,24 +110,17 @@ def tile_picked_cbn_silu_e_kernel(tc, xT, w1_words, w1_scales, gamma, beta, offs
             )
             return bank
 
-        def scale(i, bank):
+        banks = [multiply(i) for i in range(4)]
+        last_shifts = keep.tile([P, PIECE], F32, name="sheet0", align_bytes=64)
+        nc.vector.tensor_copy(last_shifts[:], beta_sb[:].indirect(entries(cls_sb, *pieces[3])))
+        for i in range(4):
             a, b = pieces[i]
-            nc.vector.tensor_tensor(scaled[:, a:b], bank[:], gains[:, a:b], ALU.mult)
-
-        banks = {i: multiply(i) for i in (1, 2)}
-        scale(1, banks[1])
-        for i in (0, 3):
-            banks[i] = multiply(i)
-        for i in (2, 0, 3):
-            scale(i, banks[i])
+            nc.vector.tensor_tensor(scaled[:, a:b], banks[i][:], gains[:, a:b], ALU.mult)
 
         for s, (a, b) in enumerate(parts):
-            shifted = keep.tile([P, b - a], F32, name="gamma_sb" if s == 0 else "shifted%d" % s, align_bytes=64)
+            shifted = keep.tile([P, b - a], F32, name="shifted%d" % s)
             result = keep.tile([P, b - a], F32, name="result%d" % s)
-            if b == S:
-                nc.vector.tensor_tensor(shifted[:], beta_sb[:].indirect(entries(cls_sb, a, b)), scaled[:, a:b], ALU.add)
-            else:
-                engine = nc.gpsimd if s == 0 else nc.vector
-                engine.tensor_tensor(shifted[:], scaled[:, a:b], shifts[:, a:b], ALU.add)
+            shift = last_shifts[:] if b == S else shifts[:, a:b]
+            nc.vector.tensor_tensor(shifted[:], scaled[:, a:b], shift, ALU.add)
             nc.scalar.activation(result[:], shifted[:], ACT.Silu, bias=zero_bias[:])
             nc.sync.dma_start(out[:, a:b], result[:])

@@ -17,7 +17,6 @@ ACT = mybir.ActivationFunctionType
 ALU = mybir.AluOpType
 
 P = 128
-HALF = 512
 PIECE = 256
 LAST = 128
 
@@ -26,7 +25,7 @@ def tile_picked_cbn_silu_e_kernel(tc, xT, w1_words, w1_scales, gamma, beta, offs
     nc = tc.nc
     x_rows = xT.rearrange("(p j) t -> p j t", j=4)
     pieces = [(a, a + PIECE) for a in range(0, S, PIECE)]
-    halves = [(a, a + HALF) for a in range(0, S, HALF)]
+    first, wide, narrow, fourth = (0, 256), (256, 640), (640, 768), (768, 1024)
 
     with ExitStack() as ctx:
         keep = ctx.enter_context(tc.tile_pool(name="keep", bufs=1))
@@ -62,65 +61,73 @@ def tile_picked_cbn_silu_e_kernel(tc, xT, w1_words, w1_scales, gamma, beta, offs
         for q in range(4):
             nc.vector.tensor_copy(w_scale[32 * q : 32 * q + 4, :].bitcast(I32), w_stage[:, q, :])
 
-        def entries(tile, a, b):
-            return tile[:, a // 16 : b // 16]
+        def entries(tile, span):
+            return tile[:, span[0] // 16 : span[1] // 16]
 
-        sheets = [keep.tile([P, PIECE, 4], BF16, name="sheet%d" % i, align_bytes=64) for i in range(len(pieces))]
+        sheets = {
+            span: keep.tile([P, span[1] - span[0], 4], BF16, name="sheet%d" % span[0], align_bytes=64)
+            for span in (first, wide, narrow, fourth)
+        }
 
         for u in range(2):
-            dense = reuse.tile([P, 2, PIECE], BF16, name="dense%d" % u, align_bytes=64, offset=(1 - u) * 4 * PIECE)
-            early = keep.tile([P, 2, HALF], BF16, name="early") if u == 0 else None
+            dense = reuse.tile([P, 2, PIECE], BF16, name="dense%d" % u, align_bytes=64, offset=(1 - u) * S)
+            small = keep.tile([P, 2, LAST], BF16, name="small%d" % u)
             for e in range(2):
                 j = 2 * u + e
-                nc.scalar.activation(dense[:, e, :], rows[j][:].indirect(entries(offs_sb, *pieces[2])), ACT.Copy)
-                if u == 0:
-                    nc.vector.tensor_copy(early[:, e, :], rows[j][:].indirect(entries(offs_sb, *halves[0])))
-                for i in ((3,), (3,), (3, 0, 1), (0, 1, 3))[j]:
-                    nc.vector.tensor_copy(sheets[i][:, :, j], rows[j][:].indirect(entries(offs_sb, *pieces[i])))
-            nc.gpsimd.tensor_scalar(sheets[2][:, :, 2 * u : 2 * u + 2], dense[:].rearrange("p e n -> p n e"), 1.0, 0.0, ALU.mult, ALU.add)
-            if u == 0:
-                for i in (0, 1):
-                    a, b = pieces[i]
-                    nc.scalar.copy(sheets[i][:, :, 0:2], early[:, :, a:b].rearrange("p e n -> p n e"))
+                nc.scalar.activation(dense[:, e, :], rows[j][:].indirect(entries(offs_sb, fourth)), ACT.Copy)
+                nc.scalar.activation(small[:, e, :], rows[j][:].indirect(entries(offs_sb, narrow)), ACT.Copy)
+                for span in (first, wide):
+                    nc.vector.tensor_copy(sheets[span][:, :, j], rows[j][:].indirect(entries(offs_sb, span)))
+            nc.gpsimd.tensor_scalar(sheets[fourth][:, :, 2 * u : 2 * u + 2], dense[:].rearrange("p e n -> p n e"), 1.0, 0.0, ALU.mult, ALU.add)
+            nc.scalar.copy(sheets[narrow][:, :, 2 * u : 2 * u + 2], small[:].rearrange("p e n -> p n e"))
 
-        def pick_table(table, name, widths):
-            pick = keep.tile([P, S], F32, name=name)
-            for a, b in widths:
-                nc.scalar.activation(pick[:, a:b], table[:].indirect(entries(cls_sb, a, b)), ACT.Copy)
-            return pick
+        gains = keep.tile([P, S], F32, name="gains")
+        shifts = keep.tile([P, S], F32, name="shifts")
 
-        gains = pick_table(gamma_sb, "gains", halves)
-        parts = [pieces[0], pieces[3], pieces[1], (HALF, HALF + LAST), (HALF + LAST, S - PIECE)]
-        shifts = pick_table(beta_sb, "shifts", pieces[:3])
-        scaled = keep.tile([P, S], F32, name="scaled")
+        def pick(dest, table, span):
+            nc.scalar.activation(dest[:, span[0] : span[1]], table[:].indirect(entries(cls_sb, span)), ACT.Copy)
 
-        def multiply(i):
-            codes = keep.tile([P, PIECE], U32, name="codes%d" % i, align_bytes=64)
-            scales = reuse.tile([P, PIECE], U8, name="scales%d" % i, align_bytes=64, offset=i * PIECE)
-            nc.vector.quantize_mx(out=codes[:].bitcast(FP8X4), scales=scales[:], in_=sheets[i][:].rearrange("p n j -> p (n j)"))
-            bank = psum.tile([P, PIECE], F32, name="bank%d" % i)
+        pick(gains, gamma_sb, pieces[0])
+        pick(gains, gamma_sb, pieces[1])
+        pick(shifts, beta_sb, pieces[0])
+        pick(gains, gamma_sb, pieces[3])
+        pick(gains, gamma_sb, pieces[2])
+        pick(shifts, beta_sb, pieces[2])
+
+        codes = keep.tile([P, S], U32, name="codes", align_bytes=64)
+        scales = reuse.tile([P, S], U8, name="scales", align_bytes=64, offset=0)
+        for span in (first, wide, fourth, narrow):
+            a, b = span
+            nc.vector.quantize_mx(out=codes[:, a:b].bitcast(FP8X4), scales=scales[:, a:b], in_=sheets[span][:].rearrange("p n j -> p (n j)"))
+
+        order = (0, 1, 3, 2)
+        banks = {}
+        for i in order:
+            a, b = pieces[i]
+            banks[i] = psum.tile([P, PIECE], F32, name="bank%d" % i)
             nc.tensor.matmul_mx(
-                out=bank[:],
+                out=banks[i][:],
                 lhsT=w_codes[:].bitcast(FP4X4),
                 lhsT_scale=w_scale[:],
-                rhs=codes[:].bitcast(FP8X4),
-                rhs_scale=scales[:],
+                rhs=codes[:, a:b].bitcast(FP8X4),
+                rhs_scale=scales[:, a:b],
                 start=True,
                 stop=True,
             )
-            return bank
-
-        banks = [multiply(i) for i in range(4)]
-        last_shifts = keep.tile([P, PIECE], F32, name="sheet0", align_bytes=64)
-        nc.vector.tensor_copy(last_shifts[:], beta_sb[:].indirect(entries(cls_sb, *pieces[3])))
-        for i in range(4):
+        scaled = keep.tile([P, S], F32, name="scaled")
+        for i in order:
             a, b = pieces[i]
             nc.vector.tensor_tensor(scaled[:, a:b], banks[i][:], gains[:, a:b], ALU.mult)
 
+        parts = [pieces[0], pieces[1], pieces[3], (512, 640), (640, 768)]
         for s, (a, b) in enumerate(parts):
             shifted = keep.tile([P, b - a], F32, name="shifted%d" % s)
             result = keep.tile([P, b - a], F32, name="result%d" % s)
-            shift = last_shifts[:] if b == S else shifts[:, a:b]
-            nc.vector.tensor_tensor(shifted[:], scaled[:, a:b], shift, ALU.add)
+            if s == 0:
+                nc.gpsimd.tensor_tensor(shifted[:], scaled[:, a:b], shifts[:, a:b], ALU.add)
+            elif s < 3:
+                nc.vector.tensor_tensor(shifted[:], beta_sb[:].indirect(entries(cls_sb, (a, b))), scaled[:, a:b], ALU.add)
+            else:
+                nc.vector.tensor_tensor(shifted[:], scaled[:, a:b], shifts[:, a:b], ALU.add)
             nc.scalar.activation(result[:], shifted[:], ACT.Silu, bias=zero_bias[:])
             nc.sync.dma_start(out[:, a:b], result[:])

@@ -37,16 +37,15 @@ def tile_picked_cbn_silu_e_kernel(tc, xT, w1_words, w1_scales, gamma, beta, offs
         w_codes = keep.tile([P, 2 * N], U8, name="w_codes", align_bytes=64)
         w_stage = keep.tile([4, 4, N // 4], I32, name="w_stage")
         w_scale = keep.tile([P, N], U8, name="w_scale", align_bytes=64)
-        nc.sync.dma_start(w_stage[:], w1_scales[0].bitcast(I32).rearrange("(q r) c -> r q c", r=4))
-        nc.sync.dma_start(offs_sb[:], offs)
-        nc.sync.dma_start(cls_sb[:], cls)
-        nc.sync.dma_start(w_codes[:].bitcast(I32), w1_words[0].bitcast(I32))
+        nc.scalar.dma_start(w_stage[:], w1_scales[0].bitcast(I32).rearrange("(q r) c -> r q c", r=4))
 
         rows = []
         for j in range(4):
             row = keep.tile([P, T], F32, name="row%d" % j)
-            nc.scalar.dma_start(row[:], x_rows[:, j, :])
+            nc.sync.dma_start(row[:], x_rows[:, j, :])
             rows.append(row)
+            if j == 0:
+                nc.sync.dma_start(offs_sb[:], offs)
         zero_in = keep.tile([P, 1], F32, name="zero_in")
         zero_bias = keep.tile([P, 1], F32, name="zero_bias")
         nc.gpsimd.memset(zero_in[:], 0.0)
@@ -54,8 +53,10 @@ def tile_picked_cbn_silu_e_kernel(tc, xT, w1_words, w1_scales, gamma, beta, offs
 
         gamma_sb = keep.tile([P, U], F32, name="gamma_sb")
         beta_sb = keep.tile([P, U], F32, name="beta_sb")
-        nc.scalar.dma_start(gamma_sb[:], gamma)
-        nc.scalar.dma_start(beta_sb[:], beta)
+        nc.sync.dma_start(cls_sb[:], cls)
+        nc.sync.dma_start(gamma_sb[:], gamma)
+        nc.sync.dma_start(w_codes[:].bitcast(I32), w1_words[0].bitcast(I32))
+        nc.sync.dma_start(beta_sb[:], beta)
 
         nc.gpsimd.memset(w_scale[:].bitcast(I32), 0)
         for q in range(4):
@@ -69,17 +70,22 @@ def tile_picked_cbn_silu_e_kernel(tc, xT, w1_words, w1_scales, gamma, beta, offs
             for span in (first, wide, narrow, fourth)
         }
 
+        thirds = ((768, 896), narrow, (896, 1024))
         for u in range(2):
-            dense = reuse.tile([P, 2, PIECE], BF16, name="dense%d" % u, align_bytes=64, offset=(1 - u) * S)
-            small = keep.tile([P, 2, LAST], BF16, name="small%d" % u)
+            dense = [
+                reuse.tile([P, 2, LAST], BF16, name="dense%d_%d" % (u, h), align_bytes=64, offset=S + 4 * LAST * (3 * u + h) if (u, h) != (1, 2) else 0)
+                for h in range(3)
+            ]
             for e in range(2):
                 j = 2 * u + e
-                nc.scalar.activation(dense[:, e, :], rows[j][:].indirect(entries(offs_sb, fourth)), ACT.Copy)
-                nc.scalar.activation(small[:, e, :], rows[j][:].indirect(entries(offs_sb, narrow)), ACT.Copy)
+                for h in range(3):
+                    nc.scalar.activation(dense[h][:, e, :], rows[j][:].indirect(entries(offs_sb, thirds[h])), ACT.Copy)
                 for span in (first, wide):
                     nc.vector.tensor_copy(sheets[span][:, :, j], rows[j][:].indirect(entries(offs_sb, span)))
-            nc.gpsimd.tensor_scalar(sheets[fourth][:, :, 2 * u : 2 * u + 2], dense[:].rearrange("p e n -> p n e"), 1.0, 0.0, ALU.mult, ALU.add)
-            nc.scalar.copy(sheets[narrow][:, :, 2 * u : 2 * u + 2], small[:].rearrange("p e n -> p n e"))
+            for h in (0, 2):
+                a = thirds[h][0] - fourth[0]
+                nc.gpsimd.tensor_scalar(sheets[fourth][:, a : a + LAST, 2 * u : 2 * u + 2], dense[h][:].rearrange("p e n -> p n e"), 1.0, 0.0, ALU.mult, ALU.add)
+            nc.scalar.copy(sheets[narrow][:, :, 2 * u : 2 * u + 2], dense[1][:].rearrange("p e n -> p n e"))
 
         gains = keep.tile([P, S], F32, name="gains")
         shifts = keep.tile([P, S], F32, name="shifts")
@@ -89,10 +95,9 @@ def tile_picked_cbn_silu_e_kernel(tc, xT, w1_words, w1_scales, gamma, beta, offs
 
         pick(gains, gamma_sb, pieces[0])
         pick(gains, gamma_sb, pieces[1])
-        pick(shifts, beta_sb, pieces[0])
         pick(gains, gamma_sb, pieces[3])
         pick(gains, gamma_sb, pieces[2])
-        pick(shifts, beta_sb, pieces[2])
+        pick(shifts, beta_sb, (pieces[1][0], pieces[2][1]))
 
         codes = keep.tile([P, S], U32, name="codes", align_bytes=64)
         scales = reuse.tile([P, S], U8, name="scales", align_bytes=64, offset=0)
@@ -114,20 +119,22 @@ def tile_picked_cbn_silu_e_kernel(tc, xT, w1_words, w1_scales, gamma, beta, offs
                 start=True,
                 stop=True,
             )
-        scaled = keep.tile([P, S], F32, name="scaled")
+        scaled = {}
         for i in order:
             a, b = pieces[i]
-            nc.vector.tensor_tensor(scaled[:, a:b], banks[i][:], gains[:, a:b], ALU.mult)
+            scaled[i] = reuse.tile([P, PIECE], F32, name="scaled%d" % i, align_bytes=64, offset=4 * S + 4 * a)
+            nc.vector.tensor_tensor(scaled[i][:], banks[i][:], gains[:, a:b], ALU.mult)
 
-        parts = [pieces[0], pieces[1], pieces[3], (512, 640), (640, 768)]
+        parts = pieces[:3] + [(768, 896), (896, 1024)]
         for s, (a, b) in enumerate(parts):
-            shifted = keep.tile([P, b - a], F32, name="shifted%d" % s)
+            i = a // PIECE
+            at = 4 * S + 4 * PIECE + 4 * (a - pieces[3][0]) if i == 3 else 8 * S + 4 * a
+            shifted = reuse.tile([P, b - a], F32, name="shifted%d" % s, align_bytes=64, offset=at)
             result = keep.tile([P, b - a], F32, name="result%d" % s)
-            if s == 0:
-                nc.gpsimd.tensor_tensor(shifted[:], scaled[:, a:b], shifts[:, a:b], ALU.add)
-            elif s < 3:
-                nc.vector.tensor_tensor(shifted[:], beta_sb[:].indirect(entries(cls_sb, (a, b))), scaled[:, a:b], ALU.add)
+            product = scaled[i][:, a - i * PIECE : b - i * PIECE]
+            if i in (0, 3):
+                nc.vector.tensor_tensor(shifted[:], beta_sb[:].indirect(entries(cls_sb, (a, b))), product, ALU.add)
             else:
-                nc.vector.tensor_tensor(shifted[:], scaled[:, a:b], shifts[:, a:b], ALU.add)
+                nc.vector.tensor_tensor(shifted[:], product, shifts[:, a:b], ALU.add)
             nc.scalar.activation(result[:], shifted[:], ACT.Silu, bias=zero_bias[:])
             nc.sync.dma_start(out[:, a:b], result[:])

@@ -37,15 +37,16 @@ def tile_picked_cbn_silu_e_kernel(tc, xT, w1_words, w1_scales, gamma, beta, offs
         w_codes = keep.tile([P, 2 * N], U8, name="w_codes", align_bytes=64)
         w_stage = keep.tile([4, 4, N // 4], I32, name="w_stage")
         w_scale = keep.tile([P, N], U8, name="w_scale", align_bytes=64)
-        nc.scalar.dma_start(w_stage[:], w1_scales[0].bitcast(I32).rearrange("(q r) c -> r q c", r=4))
+        nc.sync.dma_start(w_stage[:], w1_scales[0].bitcast(I32).rearrange("(q r) c -> r q c", r=4))
+        nc.sync.dma_start(offs_sb[:], offs)
+        nc.sync.dma_start(cls_sb[:], cls)
+        nc.sync.dma_start(w_codes[:].bitcast(I32), w1_words[0].bitcast(I32))
 
         rows = []
         for j in range(4):
             row = keep.tile([P, T], F32, name="row%d" % j)
-            nc.sync.dma_start(row[:], x_rows[:, j, :])
+            nc.scalar.dma_start(row[:], x_rows[:, j, :])
             rows.append(row)
-            if j == 0:
-                nc.sync.dma_start(offs_sb[:], offs)
         zero_in = keep.tile([P, 1], F32, name="zero_in")
         zero_bias = keep.tile([P, 1], F32, name="zero_bias")
         nc.gpsimd.memset(zero_in[:], 0.0)
@@ -53,10 +54,8 @@ def tile_picked_cbn_silu_e_kernel(tc, xT, w1_words, w1_scales, gamma, beta, offs
 
         gamma_sb = keep.tile([P, U], F32, name="gamma_sb")
         beta_sb = keep.tile([P, U], F32, name="beta_sb")
-        nc.sync.dma_start(cls_sb[:], cls)
-        nc.sync.dma_start(gamma_sb[:], gamma)
-        nc.sync.dma_start(w_codes[:].bitcast(I32), w1_words[0].bitcast(I32))
-        nc.sync.dma_start(beta_sb[:], beta)
+        nc.scalar.dma_start(gamma_sb[:], gamma)
+        nc.scalar.dma_start(beta_sb[:], beta)
 
         nc.gpsimd.memset(w_scale[:].bitcast(I32), 0)
         for q in range(4):

@@ -69,6 +69,7 @@ def tile_picked_cbn_silu_e_kernel(tc, xT, w1_words, w1_scales, gamma, beta, offs
             for span in (first, wide, narrow, fourth)
         }
 
+        early = keep.tile([P, 2, PIECE], BF16, name="early")
         thirds = ((768, 896), narrow, (896, 1024))
         for u in range(2):
             dense = [
@@ -79,11 +80,15 @@ def tile_picked_cbn_silu_e_kernel(tc, xT, w1_words, w1_scales, gamma, beta, offs
                 j = 2 * u + e
                 for h in range(3):
                     nc.scalar.activation(dense[h][:, e, :], rows[j][:].indirect(entries(offs_sb, thirds[h])), ACT.Copy)
-                for span in (first, wide):
+                if u == 0:
+                    nc.scalar.activation(early[:, e, :], rows[j][:].indirect(entries(offs_sb, first)), ACT.Copy)
+                for span in ((wide,), (wide,), (wide, first), (first, wide))[j]:
                     nc.vector.tensor_copy(sheets[span][:, :, j], rows[j][:].indirect(entries(offs_sb, span)))
             for h in (0, 2):
                 a = thirds[h][0] - fourth[0]
                 nc.gpsimd.tensor_scalar(sheets[fourth][:, a : a + LAST, 2 * u : 2 * u + 2], dense[h][:].rearrange("p e n -> p n e"), 1.0, 0.0, ALU.mult, ALU.add)
+            if u == 0:
+                nc.scalar.copy(sheets[first][:, :, 0:2], early[:].rearrange("p e n -> p n e"))
             nc.scalar.copy(sheets[narrow][:, :, 2 * u : 2 * u + 2], dense[1][:].rearrange("p e n -> p n e"))
 
         gains = keep.tile([P, S], F32, name="gains")
@@ -95,8 +100,9 @@ def tile_picked_cbn_silu_e_kernel(tc, xT, w1_words, w1_scales, gamma, beta, offs
         pick(gains, gamma_sb, pieces[0])
         pick(gains, gamma_sb, pieces[1])
         pick(gains, gamma_sb, pieces[3])
+        pick(shifts, beta_sb, pieces[0])
         pick(gains, gamma_sb, pieces[2])
-        pick(shifts, beta_sb, (pieces[1][0], pieces[2][1]))
+        pick(shifts, beta_sb, (pieces[2][0], S - LAST))
 
         codes = keep.tile([P, S], U32, name="codes", align_bytes=64)
         scales = reuse.tile([P, S], U8, name="scales", align_bytes=64, offset=0)
@@ -127,11 +133,13 @@ def tile_picked_cbn_silu_e_kernel(tc, xT, w1_words, w1_scales, gamma, beta, offs
         parts = pieces[:3] + [(768, 896), (896, 1024)]
         for s, (a, b) in enumerate(parts):
             i = a // PIECE
-            at = 4 * S + 4 * PIECE + 4 * (a - pieces[3][0]) if i == 3 else 8 * S + 4 * a
+            at = 4 * S + 4 * pieces[2][0] if b == S else 8 * S + 4 * a
             shifted = reuse.tile([P, b - a], F32, name="shifted%d" % s, align_bytes=64, offset=at)
             result = keep.tile([P, b - a], F32, name="result%d" % s)
             product = scaled[i][:, a - i * PIECE : b - i * PIECE]
-            if i in (0, 3):
+            if i == 0:
+                nc.gpsimd.tensor_tensor(shifted[:], product, shifts[:, a:b], ALU.add)
+            elif i == 1 or b == S:
                 nc.vector.tensor_tensor(shifted[:], beta_sb[:].indirect(entries(cls_sb, (a, b))), product, ALU.add)
             else:
                 nc.vector.tensor_tensor(shifted[:], product, shifts[:, a:b], ALU.add)

from contextlib import ExitStack

import concourse.mybir as mybir

K, T, S, N, U = 512, 2048, 1024, 128, 1024
FLOPS = 2 * K * N * S

F32 = mybir.dt.float32
BF16 = mybir.dt.bfloat16
I32 = mybir.dt.int32
U32 = mybir.dt.uint32
U16 = mybir.dt.uint16
U8 = mybir.dt.uint8
FP8X4 = mybir.dt.float8_e4m3fn_x4
FP4X4 = mybir.dt.float4_e2m1fn_x4
ACT = mybir.ActivationFunctionType
ALU = mybir.AluOpType

P = 128
PIECE = 256
LAST = 128


def tile_picked_cbn_silu_e_kernel(tc, xT, w1_words, w1_scales, gamma, beta, offs, cls, out):
    nc = tc.nc
    x_rows = xT.rearrange("(p j) t -> p j t", j=4)
    pieces = [(a, a + PIECE) for a in range(0, S, PIECE)]
    first, wide, narrow, fourth = (0, 256), (256, 640), (640, 768), (768, 1024)

    with ExitStack() as ctx:
        keep = ctx.enter_context(tc.tile_pool(name="keep", bufs=1))
        reuse = ctx.enter_context(tc.tile_pool(name="reuse", bufs=1))
        psum = ctx.enter_context(tc.psum_pool(name="psum", bufs=1))

        cls_sb = keep.tile([P, S // 16], U16, name="cls_sb")
        offs_sb = keep.tile([P, S // 16], U16, name="offs_sb")
        w_codes = keep.tile([P, 2 * N], U8, name="w_codes", align_bytes=64)
        w_stage = keep.tile([4, 4, N // 4], I32, name="w_stage")
        w_scale = keep.tile([P, N], U8, name="w_scale", align_bytes=64)
        nc.sync.dma_start(w_stage[:], w1_scales[0].bitcast(I32).rearrange("(q r) c -> r q c", r=4))
        nc.sync.dma_start(offs_sb[:], offs)
        nc.sync.dma_start(cls_sb[:], cls)
        nc.sync.dma_start(w_codes[:].bitcast(I32), w1_words[0].bitcast(I32))

        rows = []
        for j in range(4):
            row = keep.tile([P, T], F32, name="row%d" % j)
            nc.scalar.dma_start(row[:], x_rows[:, j, :])
            rows.append(row)
        zero_in = keep.tile([P, 1], F32, name="zero_in")
        zero_bias = keep.tile([P, 1], F32, name="zero_bias")
        nc.gpsimd.memset(zero_in[:], 0.0)
        nc.scalar.activation(zero_bias[:], zero_in[:], ACT.Silu)

        gamma_sb = keep.tile([P, U], F32, name="gamma_sb")
        beta_sb = keep.tile([P, U], F32, name="beta_sb")
        nc.scalar.dma_start(gamma_sb[:], gamma)
        nc.scalar.dma_start(beta_sb[:], beta)

        nc.gpsimd.memset(w_scale[:].bitcast(I32), 0)
        for q in range(4):
            nc.vector.tensor_copy(w_scale[32 * q : 32 * q + 4, :].bitcast(I32), w_stage[:, q, :])

        def entries(tile, span):
            return tile[:, span[0] // 16 : span[1] // 16]

        sheets = {
            span: keep.tile([P, span[1] - span[0], 4], BF16, name="sheet%d" % span[0], align_bytes=64)
            for span in (first, wide, narrow, fourth)
        }

        early = keep.tile([P, 2, PIECE], BF16, name="early")
        thirds = ((768, 896), narrow, (896, 1024))
        for u in range(2):
            dense = [
                reuse.tile([P, 2, LAST], BF16, name="dense%d_%d" % (u, h), align_bytes=64, offset=S + 4 * LAST * (3 * u + h) if (u, h) != (1, 2) else 0)
                for h in range(3)
            ]
            for e in range(2):
                j = 2 * u + e
                for h in range(3):
                    nc.scalar.activation(dense[h][:, e, :], rows[j][:].indirect(entries(offs_sb, thirds[h])), ACT.Copy)
                if u == 0:
                    nc.scalar.activation(early[:, e, :], rows[j][:].indirect(entries(offs_sb, first)), ACT.Copy)
                for span in ((wide,), (wide,), (wide, first), (first, wide))[j]:
                    nc.vector.tensor_copy(sheets[span][:, :, j], rows[j][:].indirect(entries(offs_sb, span)))
            for h in (0, 2):
                a = thirds[h][0] - fourth[0]
                nc.gpsimd.tensor_scalar(sheets[fourth][:, a : a + LAST, 2 * u : 2 * u + 2], dense[h][:].rearrange("p e n -> p n e"), 1.0, 0.0, ALU.mult, ALU.add)
            if u == 0:
                nc.scalar.copy(sheets[first][:, :, 0:2], early[:].rearrange("p e n -> p n e"))
            nc.scalar.copy(sheets[narrow][:, :, 2 * u : 2 * u + 2], dense[1][:].rearrange("p e n -> p n e"))

        gains = keep.tile([P, S], F32, name="gains")
        shifts = keep.tile([P, S], F32, name="shifts")

        def pick(dest, table, span):
            nc.scalar.activation(dest[:, span[0] : span[1]], table[:].indirect(entries(cls_sb, span)), ACT.Copy)

        pick(gains, gamma_sb, pieces[0])
        pick(gains, gamma_sb, pieces[1])
        pick(gains, gamma_sb, pieces[3])
        pick(shifts, beta_sb, pieces[0])
        pick(gains, gamma_sb, pieces[2])
        pick(shifts, beta_sb, (pieces[2][0], S - LAST))

        codes = keep.tile([P, S], U32, name="codes", align_bytes=64)
        scales = reuse.tile([P, S], U8, name="scales", align_bytes=64, offset=0)
        for span in (first, wide, fourth, narrow):
            a, b = span
            nc.vector.quantize_mx(out=codes[:, a:b].bitcast(FP8X4), scales=scales[:, a:b], in_=sheets[span][:].rearrange("p n j -> p (n j)"))

        order = (0, 1, 3, 2)
        banks = {}
        for i in order:
            a, b = pieces[i]
            banks[i] = psum.tile([P, PIECE], F32, name="bank%d" % i)
            nc.tensor.matmul_mx(
                out=banks[i][:],
                lhsT=w_codes[:].bitcast(FP4X4),
                lhsT_scale=w_scale[:],
                rhs=codes[:, a:b].bitcast(FP8X4),
                rhs_scale=scales[:, a:b],
                start=True,
                stop=True,
            )
        scaled = {}
        for i in order:
            a, b = pieces[i]
            scaled[i] = reuse.tile([P, PIECE], F32, name="scaled%d" % i, align_bytes=64, offset=4 * S + 4 * a)
            nc.vector.tensor_tensor(scaled[i][:], banks[i][:], gains[:, a:b], ALU.mult)

        parts = pieces[:3] + [(768, 896), (896, 1024)]
        for s, (a, b) in enumerate(parts):
            i = a // PIECE
            at = 4 * S + 4 * pieces[2][0] if b == S else 8 * S + 4 * a
            shifted = reuse.tile([P, b - a], F32, name="shifted%d" % s, align_bytes=64, offset=at)
            result = keep.tile([P, b - a], F32, name="result%d" % s)
            product = scaled[i][:, a - i * PIECE : b - i * PIECE]
            if i == 0:
                nc.gpsimd.tensor_tensor(shifted[:], product, shifts[:, a:b], ALU.add)
            elif i == 1 or b == S:
                nc.vector.tensor_tensor(shifted[:], beta_sb[:].indirect(entries(cls_sb, (a, b))), product, ALU.add)
            else:
                nc.vector.tensor_tensor(shifted[:], product, shifts[:, a:b], ALU.add)
            nc.scalar.activation(result[:], shifted[:], ACT.Silu, bias=zero_bias[:])
            nc.sync.dma_start(out[:, a:b], result[:])
